import numpy as np
import ml_dtypes


def mxq(x, axis, fmt="e4m3"):
    dtype, down = {"e4m3": (ml_dtypes.float8_e4m3fn, 7), "e5m2": (ml_dtypes.float8_e5m2, 14)}[fmt]
    v = np.moveaxis(np.asarray(x, np.float32).astype(ml_dtypes.bfloat16).astype(np.float64), axis, -1)
    blocks = v.reshape(v.shape[:-1] + (-1, 32))
    amax = np.abs(blocks).max(-1, keepdims=True)
    byte = np.maximum(np.where(amax > 0, np.frexp(amax)[1] - 1 + 127, 0) - down, 1)
    scale = np.exp2(byte - 127.0)
    codes = (blocks / scale).astype(np.float32).astype(dtype).astype(np.float64)
    return np.moveaxis((codes * scale).reshape(v.shape), -1, axis)


WIDE = False


def mx_kscale(k):
    if not WIDE:
        return np.ones(k)
    levels = np.array([10, -10, 5, -5, 0])
    if k % 512:
        return np.exp2(np.random.permutation(np.resize(levels, k // 32))).repeat(32)
    a = np.empty((k // 512, 16))
    for p in range(k // 512):
        a[p, :8] = np.random.permutation(np.resize(levels, 8))
        for g in range(8):
            far = levels[np.abs(levels - a[p, g]) >= 10]
            a[p, g + 8] = far[np.random.randint(len(far))]
    return np.exp2(a.ravel()).repeat(32)


def f64(x):
    return np.asarray(x).astype(np.float64)


def striped(idx):
    return np.tile(idx.reshape(-1, 16).T, (8, 1)).astype(np.uint16)


def unstriped(offs):
    return offs[:16].T.reshape(-1).astype(np.int64)


def sigmoid(v):
    return 1.0 / (1.0 + np.exp(-np.maximum(v, -700.0)))


K, T, S, N = 512, 2048, 1024, 256


def setup_inputs():
    n = np.random.standard_normal
    s = mx_kscale(K)[:, None]
    return {
        "xT": (n((K, T)) * s).astype(np.float32),
        "res": n((N, T)).astype(np.float32),
        "w1": (n((K, N)) / np.sqrt(K) / s).astype(np.float32),
        "w2": (n((K, N)) / np.sqrt(K) / s).astype(np.float32),
        "offs": striped(np.random.permutation(T)[:S]),
    }


def reference(xT, res, w1, w2, offs):
    r = f64(res)[:, unstriped(offs)]
    xq = mxq(f64(xT)[:, unstriped(offs)], 0, "e4m3")
    g = sigmoid(mxq(f64(w2), 0, "e4m3").T @ xq)
    y = np.tanh(mxq(f64(w1), 0, "e4m3").T @ xq)
    return r + g * (y - r)

@@ -1,0 +1,197 @@
+from contextlib import ExitStack
+
+import concourse.mybir as mybir
+
+K, T, S, N = 512, 2048, 1024, 256
+FLOPS = 2 * 2 * K * N * S
+
+F32 = mybir.dt.float32
+BF16 = mybir.dt.bfloat16
+U32 = mybir.dt.uint32
+U16 = mybir.dt.uint16
+U8 = mybir.dt.uint8
+FP8X4 = mybir.dt.float8_e4m3fn_x4
+ACT = mybir.ActivationFunctionType
+ALU = mybir.AluOpType
+
+P = 128
+PACK = 4
+LIST_ROWS = 16
+CHUNK = 256
+HALF = 512
+
+
+def tile_picked_highway_tanh_l_kernel(tc, xT, res, w1, w2, offs, out):
+    nc = tc.nc
+    x_rows = xT.rearrange("(p j) t -> p j t", j=PACK)
+
+    with ExitStack() as ctx:
+        keep = ctx.enter_context(tc.tile_pool(name="keep", bufs=1))
+        psum = ctx.enter_context(tc.psum_pool(name="psum", bufs=1))
+
+        offsets = keep.tile([P, S // LIST_ROWS], U16, name="offsets")
+
+        def entries(a, b):
+            return offsets[:, a // LIST_ROWS : b // LIST_ROWS]
+
+        warm_in = keep.tile([P, 8], F32, name="warm_in")
+        warm_out = keep.tile([P, 8], F32, name="warm_out")
+        nc.gpsimd.memset(warm_in[:], 0.0)
+        nc.scalar.activation(warm_out[:], warm_in[:], ACT.Sigmoid)
+
+        x_loads = [(0, 0, 1024), (0, 1024, 2048), (1, 0, 1024), (1, 1024, 1536), (1, 1536, 2048)]
+        x_raw = []
+        for i, (u, a, b) in enumerate(x_loads):
+            raw = keep.tile([P, 2, b - a], F32, name="x_raw%d" % i)
+            nc.sync.dma_start(out=raw[:], in_=x_rows[:, 2 * u : 2 * u + 2, a:b])
+            x_raw.append(raw)
+            if i == 1:
+                nc.sync.dma_start(offsets[:], offs)
+        w_raw = []
+        for i, w in enumerate((w2, w1)):
+            raw = keep.tile([P, PACK, N], F32, name="w_raw%d" % i)
+            nc.sync.dma_start(out=raw[:], in_=w.rearrange("(p j) n -> p j n", j=PACK))
+            w_raw.append(raw)
+        res_rows = []
+        for mt in range(N // P):
+            r = keep.tile([P, T], F32, name="res%d" % mt)
+            nc.sync.dma_start(out=r[:], in_=res[mt * P : (mt + 1) * P, :])
+            res_rows.append(r)
+
+        pairs = [keep.tile([P, T, 2], BF16, name="pairs%d" % u) for u in range(2)]
+
+        def cast(engine, i, a, b):
+            u, a0, b0 = x_loads[i]
+            src = x_raw[i][:, :, a:b].rearrange("p j c -> p c j")
+            dst = pairs[u][:, a0 + a : a0 + b, :]
+            if engine == "v":
+                nc.vector.tensor_copy(out=dst, in_=src)
+            else:
+                nc.scalar.copy(out=dst, in_=src)
+
+        words = [pairs[u][:].rearrange("p t j -> p (t j)").bitcast(U32) for u in range(2)]
+        picked = [keep.tile([P, 2, CHUNK], U32, name="picked%d" % c) for c in range(S // CHUNK)]
+        woven = [keep.tile([P, CHUNK, PACK], BF16, name="woven%d" % c, align_bytes=64) for c in range(S // CHUNK)]
+        x_codes = [keep.tile([P, HALF], U32, name="x_codes%d" % h, align_bytes=64) for h in range(S // HALF)]
+        x_scales = [keep.tile([P, HALF], U8, name="x_scales%d" % h, align_bytes=64) for h in range(S // HALF)]
+
+        def gather_x(u, c):
+            nc.vector.tensor_copy(out=picked[c][:, u, :], in_=words[u].indirect(entries(c * CHUNK, (c + 1) * CHUNK)))
+
+        def weave(c):
+            dst = woven[c][:].rearrange("p n j -> p (n j)").bitcast(U32).rearrange("p (n u) -> p n u", u=2)
+            nc.scalar.copy(out=dst, in_=picked[c][:].rearrange("p u n -> p n u"))
+
+        def quantize_x(c):
+            h, a = divmod(c * CHUNK, HALF)
+            nc.vector.quantize_mx(
+                out=x_codes[h][:, a : a + CHUNK].bitcast(FP8X4),
+                scales=x_scales[h][:, a : a + CHUNK],
+                in_=woven[c][:].rearrange("p n j -> p (n j)"),
+            )
+
+        cast("s", 0, 0, 1024)
+        cast("v", 1, 0, 704)
+        cast("s", 1, 704, 1024)
+        for c in range(4):
+            gather_x(0, c)
+        cast("s", 2, 0, 1024)
+        cast("v", 3, 0, 512)
+        cast("v", 4, 0, 352)
+        cast("s", 4, 352, 512)
+
+        w_grouped = [keep.tile([P, N, PACK], BF16, name="w_grouped%d" % i, align_bytes=64) for i in range(2)]
+        w_codes = [keep.tile([P, N], U32, name="w_codes%d" % i, align_bytes=64) for i in range(2)]
+        w_scales = [keep.tile([P, N], U8, name="w_scales%d" % i, align_bytes=64) for i in range(2)]
+
+        def group_w(engine, i):
+            dst = w_grouped[i][:].rearrange("p (c i) t -> p c t i", i=4)
+            src = w_raw[i][:].rearrange("p t (c i) -> p c t i", i=4)
+            if engine == "v":
+                nc.vector.tensor_copy(out=dst, in_=src)
+            else:
+                nc.scalar.copy(out=dst, in_=src)
+
+        def quantize_w(i):
+            nc.vector.quantize_mx(
+                out=w_codes[i][:].bitcast(FP8X4),
+                scales=w_scales[i][:],
+                in_=w_grouped[i][:].rearrange("p n j -> p (n j)"),
+            )
+
+        gather_x(1, 0)
+        gather_x(1, 1)
+        weave(0)
+        weave(1)
+        gather_x(1, 2)
+        quantize_x(0)
+        group_w("s", 0)
+        gather_x(1, 3)
+        quantize_x(1)
+        weave(2)
+        weave(3)
+        quantize_w(0)
+        group_w("v", 1)
+        quantize_x(2)
+        quantize_w(1)
+        quantize_x(3)
+
+        units = [(mt, h) for mt in range(N // P) for h in range(S // HALF)]
+        acts = {}
+        for mt, h in units:
+            for i in range(2):
+                acc = psum.tile([P, HALF], F32, name="acc%d%d%d" % (mt, h, i))
+                nc.tensor.matmul_mx(
+                    out=acc[:],
+                    lhsT=w_codes[i][:, mt * P : (mt + 1) * P].bitcast(FP8X4),
+                    lhsT_scale=w_scales[i][:, mt * P : (mt + 1) * P],
+                    rhs=x_codes[h][:].bitcast(FP8X4),
+                    rhs_scale=x_scales[h][:],
+                    start=True,
+                    stop=True,
+                )
+                val = keep.tile([P, HALF], F32, name="act%d%d%d" % (mt, h, i))
+                if i == 0:
+                    nc.scalar.activation(val[:], acc[:], ACT.Sigmoid, scale=-1.0)
+                else:
+                    nc.scalar.activation(val[:], acc[:], ACT.Tanh)
+                acts[mt, h, i] = val
+
+        pieces = [(0, 0, 512), (0, 512, 1024), (1, 0, 512), (1, 512, 768), (1, 768, 1024)]
+        carried, fresh = {}, {}
+
+        def carry(n):
+            mt, a, b = pieces[n]
+            h, o = divmod(a, HALF)
+            q = keep.tile([P, b - a], F32, name="carried%d" % n)
+            nc.vector.tensor_tensor(q[:], res_rows[mt][:].indirect(entries(a, b)), acts[mt, h, 0][:, o : o + b - a], ALU.mult)
+            carried[n] = q
+
+        def gate(mt, h):
+            g = keep.tile([P, HALF], F32, name="fresh%d%d" % (mt, h))
+            nc.vector.scalar_tensor_tensor(
+                out=g[:], in0=acts[mt, h, 0][:], scalar=-1.0, in1=acts[mt, h, 1][:], op0=ALU.add, op1=ALU.mult
+            )
+            fresh[mt, h] = g
+
+        def finish(n):
+            mt, a, b = pieces[n]
+            h, o = divmod(a, HALF)
+            y = keep.tile([P, b - a], F32, name="result%d" % n)
+            nc.vector.tensor_tensor(y[:], carried[n][:], fresh[mt, h][:, o : o + b - a], ALU.subtract)
+            nc.sync.dma_start(out=out[mt * P : (mt + 1) * P, a:b], in_=y[:])
+
+        carry(0)
+        gate(0, 0)
+        carry(1)
+        finish(0)
+        gate(0, 1)
+        gate(1, 0)
+        finish(1)
+        carry(2)
+        gate(1, 1)
+        finish(2)
+        carry(3)
+        carry(4)
+        finish(3)
+        finish(4)

@@ -1,6 +1,7 @@
 from contextlib import ExitStack
 
 import concourse.mybir as mybir
+from concourse.masks import make_identity
 
 K, T, S, N = 512, 2048, 1024, 256
 FLOPS = 2 * 2 * K * N * S
@@ -8,6 +9,7 @@ FLOPS = 2 * 2 * K * N * S
 F32 = mybir.dt.float32
 BF16 = mybir.dt.bfloat16
 U32 = mybir.dt.uint32
+I32 = mybir.dt.int32
 U16 = mybir.dt.uint16
 U8 = mybir.dt.uint8
 FP8X4 = mybir.dt.float8_e4m3fn_x4
@@ -19,6 +21,7 @@ PACK = 4
 LIST_ROWS = 16
 CHUNK = 256
 HALF = 512
+BLOCKS = HALF // P
 
 
 def tile_picked_highway_tanh_l_kernel(tc, xT, res, w1, w2, offs, out):
@@ -27,7 +30,7 @@ def tile_picked_highway_tanh_l_kernel(tc, xT, res, w1, w2, offs, out):
 
     with ExitStack() as ctx:
         keep = ctx.enter_context(tc.tile_pool(name="keep", bufs=1))
-        psum = ctx.enter_context(tc.psum_pool(name="psum", bufs=1))
+        psum = ctx.enter_context(tc.psum_pool(name="psum", bufs=4))
 
         offsets = keep.tile([P, S // LIST_ROWS], U16, name="offsets")
 
@@ -36,8 +39,10 @@ def tile_picked_highway_tanh_l_kernel(tc, xT, res, w1, w2, offs, out):
 
         warm_in = keep.tile([P, 8], F32, name="warm_in")
         warm_out = keep.tile([P, 8], F32, name="warm_out")
-        nc.gpsimd.memset(warm_in[:], 0.0)
+        nc.vector.memset(warm_in[:], 0.0)
         nc.scalar.activation(warm_out[:], warm_in[:], ACT.Sigmoid)
+        ident = keep.tile([P, P], F32, name="ident")
+        make_identity(nc, ident[:])
 
         x_loads = [(0, 0, 1024), (0, 1024, 2048), (1, 0, 1024), (1, 1024, 1536), (1, 1536, 2048)]
         x_raw = []
@@ -45,18 +50,14 @@ def tile_picked_highway_tanh_l_kernel(tc, xT, res, w1, w2, offs, out):
             raw = keep.tile([P, 2, b - a], F32, name="x_raw%d" % i)
             nc.sync.dma_start(out=raw[:], in_=x_rows[:, 2 * u : 2 * u + 2, a:b])
             x_raw.append(raw)
-            if i == 1:
+            if i == 0:
                 nc.sync.dma_start(offsets[:], offs)
-        w_raw = []
+        res_rows = [keep.tile([P, T], F32, name="res%d" % mt, tag="res%d" % mt) for mt in range(2)]
+        w_raw = [keep.tile([P, PACK, N], F32, name="w_raw%d" % i) for i in range(2)]
         for i, w in enumerate((w2, w1)):
-            raw = keep.tile([P, PACK, N], F32, name="w_raw%d" % i)
-            nc.sync.dma_start(out=raw[:], in_=w.rearrange("(p j) n -> p j n", j=PACK))
-            w_raw.append(raw)
-        res_rows = []
-        for mt in range(N // P):
-            r = keep.tile([P, T], F32, name="res%d" % mt)
-            nc.sync.dma_start(out=r[:], in_=res[mt * P : (mt + 1) * P, :])
-            res_rows.append(r)
+            nc.sync.dma_start(out=w_raw[i][:], in_=w.rearrange("(p j) n -> p j n", j=PACK))
+        for mt in range(2):
+            nc.sync.dma_start(out=res_rows[mt][:], in_=res[mt * P : (mt + 1) * P, :])
 
         pairs = [keep.tile([P, T, 2], BF16, name="pairs%d" % u) for u in range(2)]
 
@@ -70,47 +71,39 @@ def tile_picked_highway_tanh_l_kernel(tc, xT, res, w1, w2, offs, out):
                 nc.scalar.copy(out=dst, in_=src)
 
         words = [pairs[u][:].rearrange("p t j -> p (t j)").bitcast(U32) for u in range(2)]
-        picked = [keep.tile([P, 2, CHUNK], U32, name="picked%d" % c) for c in range(S // CHUNK)]
-        woven = [keep.tile([P, CHUNK, PACK], BF16, name="woven%d" % c, align_bytes=64) for c in range(S // CHUNK)]
-        x_codes = [keep.tile([P, HALF], U32, name="x_codes%d" % h, align_bytes=64) for h in range(S // HALF)]
-        x_scales = [keep.tile([P, HALF], U8, name="x_scales%d" % h, align_bytes=64) for h in range(S // HALF)]
+        picked = keep.tile([P, 2, S], U32, name="picked")
+        woven = [keep.tile([P, HALF, PACK], BF16, name="woven%d" % h, align_bytes=64) for h in range(2)]
+        x_codes = [keep.tile([P, HALF], U32, name="x_codes%d" % h, align_bytes=64) for h in range(2)]
+        x_scales = [keep.tile([P, HALF], U8, name="x_scales%d" % h, align_bytes=64) for h in range(2)]
 
-        def gather_x(u, c):
-            nc.vector.tensor_copy(out=picked[c][:, u, :], in_=words[u].indirect(entries(c * CHUNK, (c + 1) * CHUNK)))
+        def gather_x(u, a, b):
+            nc.vector.tensor_copy(out=picked[:, u, a:b], in_=words[u].indirect(entries(a, b)))
 
-        def weave(c):
-            dst = woven[c][:].rearrange("p n j -> p (n j)").bitcast(U32).rearrange("p (n u) -> p n u", u=2)
-            nc.scalar.copy(out=dst, in_=picked[c][:].rearrange("p u n -> p n u"))
+        def weave(engine, a, b):
+            h, o = divmod(a, HALF)
+            dst = woven[h][:].rearrange("p n j -> p (n j)").bitcast(U32).rearrange("p (n u) -> p n u", u=2)
+            src = picked[:, :, a:b].rearrange("p u n -> p n u")
+            if engine == "v":
+                flat = woven[h][:].rearrange("p n j -> p (n j)").bitcast(I32).rearrange("p (n u) -> p n u", u=2)
+                nc.vector.tensor_copy(
+                    out=flat[:, o : o + b - a, :], in_=picked[:].bitcast(I32)[:, :, a:b].rearrange("p u n -> p n u")
+                )
+            else:
+                nc.scalar.copy(out=dst[:, o : o + b - a, :], in_=src)
 
-        def quantize_x(c):
-            h, a = divmod(c * CHUNK, HALF)
+        def quantize_x(h):
             nc.vector.quantize_mx(
-                out=x_codes[h][:, a : a + CHUNK].bitcast(FP8X4),
-                scales=x_scales[h][:, a : a + CHUNK],
-                in_=woven[c][:].rearrange("p n j -> p (n j)"),
+                out=x_codes[h][:].bitcast(FP8X4),
+                scales=x_scales[h][:],
+                in_=woven[h][:].rearrange("p n j -> p (n j)"),
             )
-
-        cast("s", 0, 0, 1024)
-        cast("v", 1, 0, 704)
-        cast("s", 1, 704, 1024)
-        for c in range(4):
-            gather_x(0, c)
-        cast("s", 2, 0, 1024)
-        cast("v", 3, 0, 512)
-        cast("v", 4, 0, 352)
-        cast("s", 4, 352, 512)
 
         w_grouped = [keep.tile([P, N, PACK], BF16, name="w_grouped%d" % i, align_bytes=64) for i in range(2)]
         w_codes = [keep.tile([P, N], U32, name="w_codes%d" % i, align_bytes=64) for i in range(2)]
         w_scales = [keep.tile([P, N], U8, name="w_scales%d" % i, align_bytes=64) for i in range(2)]
 
-        def group_w(engine, i):
-            dst = w_grouped[i][:].rearrange("p (c i) t -> p c t i", i=4)
-            src = w_raw[i][:].rearrange("p t (c i) -> p c t i", i=4)
-            if engine == "v":
-                nc.vector.tensor_copy(out=dst, in_=src)
-            else:
-                nc.scalar.copy(out=dst, in_=src)
+        def group_w(i):
+            nc.scalar.copy(out=w_grouped[i][:], in_=w_raw[i][:].rearrange("p t c -> p c t"))
 
         def quantize_w(i):
             nc.vector.quantize_mx(
@@ -119,79 +112,150 @@ def tile_picked_highway_tanh_l_kernel(tc, xT, res, w1, w2, offs, out):
                 in_=w_grouped[i][:].rearrange("p n j -> p (n j)"),
             )
 
-        gather_x(1, 0)
-        gather_x(1, 1)
-        weave(0)
-        weave(1)
-        gather_x(1, 2)
-        quantize_x(0)
-        group_w("s", 0)
-        gather_x(1, 3)
-        quantize_x(1)
-        weave(2)
-        weave(3)
-        quantize_w(0)
-        group_w("v", 1)
-        quantize_x(2)
-        quantize_w(1)
-        quantize_x(3)
+        vals = {}
 
-        units = [(mt, h) for mt in range(N // P) for h in range(S // HALF)]
-        acts = {}
-        for mt, h in units:
-            for i in range(2):
-                acc = psum.tile([P, HALF], F32, name="acc%d%d%d" % (mt, h, i))
+        def by_feature(i, mt, h, func, scale):
+            acc = psum.tile([P, HALF], F32, name="acc", tag="acc")
+            nc.tensor.matmul_mx(
+                out=acc[:],
+                lhsT=w_codes[i][:, mt * P : (mt + 1) * P].bitcast(FP8X4),
+                lhsT_scale=w_scales[i][:, mt * P : (mt + 1) * P],
+                rhs=x_codes[h][:].bitcast(FP8X4),
+                rhs_scale=x_scales[h][:],
+                start=True,
+                stop=True,
+            )
+            v = keep.tile([P, HALF], F32, name="val%d%d%d" % (i, mt, h))
+            nc.scalar.activation(v[:], acc[:], func, scale=scale)
+            vals[i, mt, h] = v
+
+        def by_token(h):
+            acc = psum.tile([P, HALF], F32, name="acc", tag="acc")
+            for t in range(BLOCKS):
+                cols = slice(t * P, (t + 1) * P)
                 nc.tensor.matmul_mx(
-                    out=acc[:],
-                    lhsT=w_codes[i][:, mt * P : (mt + 1) * P].bitcast(FP8X4),
-                    lhsT_scale=w_scales[i][:, mt * P : (mt + 1) * P],
-                    rhs=x_codes[h][:].bitcast(FP8X4),
-                    rhs_scale=x_scales[h][:],
+                    out=acc[:, cols],
+                    lhsT=x_codes[h][:, cols].bitcast(FP8X4),
+                    lhsT_scale=x_scales[h][:, cols],
+                    rhs=w_codes[0][:, 0:P].bitcast(FP8X4),
+                    rhs_scale=w_scales[0][:, 0:P],
                     start=True,
                     stop=True,
                 )
-                val = keep.tile([P, HALF], F32, name="act%d%d%d" % (mt, h, i))
-                if i == 0:
-                    nc.scalar.activation(val[:], acc[:], ACT.Sigmoid, scale=-1.0)
-                else:
-                    nc.scalar.activation(val[:], acc[:], ACT.Tanh)
-                acts[mt, h, i] = val
+            v = keep.tile([P, HALF], F32, name="gate_t%d" % h)
+            nc.scalar.activation(v[:], acc[:], ACT.Sigmoid)
+            vals[0, 0, h] = v
 
-        pieces = [(0, 0, 512), (0, 512, 1024), (1, 0, 512), (1, 512, 768), (1, 768, 1024)]
+        def turn(sources):
+            bank = psum.tile([P, HALF], F32, name="turned", tag="turned")
+            for n, src in enumerate(sources):
+                for t in range(BLOCKS):
+                    cols = slice(t * P, (t + 1) * P)
+                    nc.tensor.matmul(
+                        bank[:, cols], src[:, cols], ident[:], is_transpose=True,
+                        start=(n == 0 and t == 0), stop=(n == len(sources) - 1 and t == BLOCKS - 1),
+                    )
+            return bank
+
+        passed, passed_t, pull = {}, {}, {}
+
+        def look_up(h):
+            r = keep.tile([P, HALF], F32, name="passed%d" % h)
+            nc.vector.tensor_copy(out=r[:], in_=res_rows[0][:].indirect(entries(h * HALF, (h + 1) * HALF)))
+            passed[h] = r
+
+        def turn_passed(h):
+            rt = keep.tile([P, HALF], F32, name="passed_t%d" % h)
+            nc.scalar.copy(out=rt[:], in_=turn([passed[h]])[:])
+            passed_t[h] = rt
+
+        diff = {}
+
+        def difference(h):
+            diff[h] = turn([passed[h], vals[1, 0, h]])
+
+        def weigh(h):
+            d = diff[h]
+            e_tile = keep.tile([P, HALF], F32, name="pull%d" % h)
+            e = e_tile[:]
+            nc.vector.scalar_tensor_tensor(out=e, in0=d[:], scalar=-1.0, in1=vals[0, 0, h][:], op0=ALU.mult, op1=ALU.mult)
+            pull[h] = e
+
+        def finish_low(h):
+            y = keep.tile([P, HALF], F32, name="low%d" % h)
+            nc.scalar.copy(out=y[:], in_=turn([passed_t[h], pull[h]])[:])
+            nc.sync.dma_start(out=out[0:P, h * HALF : (h + 1) * HALF], in_=y[:])
+
+        def finish_low_v(h):
+            y = keep.tile([P, HALF], F32, name="low%d" % h)
+            nc.vector.tensor_tensor(y[:], turn([pull[h]])[:], passed[h][:], ALU.add)
+            nc.sync.dma_start(out=out[0:P, h * HALF : (h + 1) * HALF], in_=y[:])
+
         carried, fresh = {}, {}
 
-        def carry(n):
-            mt, a, b = pieces[n]
+        def carry(a, b):
             h, o = divmod(a, HALF)
-            q = keep.tile([P, b - a], F32, name="carried%d" % n)
-            nc.vector.tensor_tensor(q[:], res_rows[mt][:].indirect(entries(a, b)), acts[mt, h, 0][:, o : o + b - a], ALU.mult)
-            carried[n] = q
+            q = keep.tile([P, b - a], F32, name="carried%d" % a)
+            nc.vector.tensor_tensor(q[:], res_rows[1][:].indirect(entries(a, b)), vals[0, 1, h][:, o : o + b - a], ALU.mult)
+            carried[h] = q
 
-        def gate(mt, h):
-            g = keep.tile([P, HALF], F32, name="fresh%d%d" % (mt, h))
+        def gate(h):
+            g = keep.tile([P, HALF], F32, name="fresh%d" % h)
             nc.vector.scalar_tensor_tensor(
-                out=g[:], in0=acts[mt, h, 0][:], scalar=-1.0, in1=acts[mt, h, 1][:], op0=ALU.add, op1=ALU.mult
+                out=g[:], in0=vals[0, 1, h][:], scalar=-1.0, in1=vals[1, 1, h][:], op0=ALU.add, op1=ALU.mult
             )
-            fresh[mt, h] = g
+            fresh[h] = g
 
-        def finish(n):
-            mt, a, b = pieces[n]
+        def finish_high(a, b):
             h, o = divmod(a, HALF)
-            y = keep.tile([P, b - a], F32, name="result%d" % n)
-            nc.vector.tensor_tensor(y[:], carried[n][:], fresh[mt, h][:, o : o + b - a], ALU.subtract)
-            nc.sync.dma_start(out=out[mt * P : (mt + 1) * P, a:b], in_=y[:])
+            y = keep.tile([P, b - a], F32, name="high%d" % a)
+            nc.vector.tensor_tensor(y[:], carried[h][:, o : o + b - a], fresh[h][:, o : o + b - a], ALU.subtract)
+            nc.sync.dma_start(out=out[P : 2 * P, a:b], in_=y[:])
 
-        carry(0)
-        gate(0, 0)
-        carry(1)
-        finish(0)
-        gate(0, 1)
-        gate(1, 0)
-        finish(1)
-        carry(2)
-        gate(1, 1)
-        finish(2)
-        carry(3)
-        carry(4)
-        finish(3)
-        finish(4)
+        cast("s", 0, 0, 1024)
+        cast("v", 1, 0, 704)
+        cast("s", 1, 704, 1024)
+        gather_x(0, 0, S)
+        cast("s", 2, 0, 1024)
+        cast("v", 3, 0, 512)
+        cast("v", 4, 0, 320)
+        cast("s", 4, 320, 512)
+        gather_x(1, 0, 256)
+        weave("s", 0, 256)
+        group_w(0)
+        gather_x(1, 256, 512)
+        weave("s", 256, 512)
+        gather_x(1, 512, 768)
+        weave("s", 512, 768)
+        gather_x(1, 768, 1024)
+        group_w(1)
+        weave("v", 768, 1024)
+        quantize_w(0)
+        quantize_x(0)
+        quantize_x(1)
+        quantize_w(1)
+        look_up(0)
+        look_up(1)
+        by_feature(0, 1, 0, ACT.Sigmoid, -1.0)
+        by_feature(0, 1, 1, ACT.Sigmoid, -1.0)
+        by_feature(1, 0, 0, ACT.Tanh, -1.0)
+        by_token(0)
+        turn_passed(0)
+        by_feature(1, 0, 1, ACT.Tanh, -1.0)
+        by_token(1)
+        turn_passed(1)
+        carry(0, 512)
+        carry(512, 1024)
+        difference(0)
+        difference(1)
+        by_feature(1, 1, 0, ACT.Tanh, 1.0)
+        by_feature(1, 1, 1, ACT.Tanh, 1.0)
+        weigh(0)
+        weigh(1)
+        finish_low(0)
+        finish_low(1)
+        gate(0)
+        gate(1)
+        finish_high(0, 512)
+        finish_high(512, 768)
+        finish_high(768, 1024)

@@ -53,11 +53,10 @@ def tile_picked_highway_tanh_l_kernel(tc, xT, res, w1, w2, offs, out):
             if i == 0:
                 nc.sync.dma_start(offsets[:], offs)
         res_rows = [keep.tile([P, T], F32, name="res%d" % mt, tag="res%d" % mt) for mt in range(2)]
-        w_raw = [keep.tile([P, PACK, N], F32, name="w_raw%d" % i) for i in range(2)]
+        w_raw = [keep.tile([P, PACK, N], F32, name="w_raw%d" % i, tag="w_raw%d" % i, align_bytes=64) for i in range(2)]
         for i, w in enumerate((w2, w1)):
             nc.sync.dma_start(out=w_raw[i][:], in_=w.rearrange("(p j) n -> p j n", j=PACK))
-        for mt in range(2):
-            nc.sync.dma_start(out=res_rows[mt][:], in_=res[mt * P : (mt + 1) * P, :])
+            nc.sync.dma_start(out=res_rows[i][:], in_=res[i * P : (i + 1) * P, :])
 
         pairs = [keep.tile([P, T, 2], BF16, name="pairs%d" % u) for u in range(2)]
 
@@ -72,7 +71,7 @@ def tile_picked_highway_tanh_l_kernel(tc, xT, res, w1, w2, offs, out):
 
         words = [pairs[u][:].rearrange("p t j -> p (t j)").bitcast(U32) for u in range(2)]
         picked = keep.tile([P, 2, S], U32, name="picked")
-        woven = [keep.tile([P, HALF, PACK], BF16, name="woven%d" % h, align_bytes=64) for h in range(2)]
+        woven = {}
         x_codes = [keep.tile([P, HALF], U32, name="x_codes%d" % h, align_bytes=64) for h in range(2)]
         x_scales = [keep.tile([P, HALF], U8, name="x_scales%d" % h, align_bytes=64) for h in range(2)]
 
@@ -81,6 +80,8 @@ def tile_picked_highway_tanh_l_kernel(tc, xT, res, w1, w2, offs, out):
 
         def weave(engine, a, b):
             h, o = divmod(a, HALF)
+            if o == 0:
+                woven[h] = keep.tile([P, HALF, PACK], BF16, name="woven%d" % h, tag=("woven0", "w_raw0")[h], align_bytes=64)
             dst = woven[h][:].rearrange("p n j -> p (n j)").bitcast(U32).rearrange("p (n u) -> p n u", u=2)
             src = picked[:, :, a:b].rearrange("p u n -> p n u")
             if engine == "v":
@@ -193,24 +194,27 @@ def tile_picked_highway_tanh_l_kernel(tc, xT, res, w1, w2, offs, out):
 
         carried, fresh = {}, {}
 
-        def carry(a, b):
-            h, o = divmod(a, HALF)
-            q = keep.tile([P, b - a], F32, name="carried%d" % a)
-            nc.vector.tensor_tensor(q[:], res_rows[1][:].indirect(entries(a, b)), vals[0, 1, h][:, o : o + b - a], ALU.mult)
-            carried[h] = q
-
-        def gate(h):
-            g = keep.tile([P, HALF], F32, name="fresh%d" % h)
-            nc.vector.scalar_tensor_tensor(
-                out=g[:], in0=vals[0, 1, h][:], scalar=-1.0, in1=vals[1, 1, h][:], op0=ALU.add, op1=ALU.mult
+        def carry(mt, h):
+            q = keep.tile([P, HALF], F32, name="carried%d%d" % (mt, h))
+            nc.vector.tensor_tensor(
+                q[:], res_rows[mt][:].indirect(entries(h * HALF, (h + 1) * HALF)), vals[0, mt, h][:], ALU.mult
             )
-            fresh[h] = g
+            carried[mt, h] = q
 
-        def finish_high(a, b):
+        def gate(mt, a, b):
             h, o = divmod(a, HALF)
-            y = keep.tile([P, b - a], F32, name="high%d" % a)
-            nc.vector.tensor_tensor(y[:], carried[h][:, o : o + b - a], fresh[h][:, o : o + b - a], ALU.subtract)
-            nc.sync.dma_start(out=out[P : 2 * P, a:b], in_=y[:])
+            cols = slice(o, o + b - a)
+            g = keep.tile([P, b - a], F32, name="fresh%d_%d" % (mt, a))
+            nc.vector.scalar_tensor_tensor(
+                out=g[:], in0=vals[0, mt, h][:, cols], scalar=-1.0, in1=vals[1, mt, h][:, cols], op0=ALU.add, op1=ALU.mult
+            )
+            fresh[mt, a] = g
+
+        def finish(mt, a, b):
+            h, o = divmod(a, HALF)
+            y = keep.tile([P, b - a], F32, name="result%d_%d" % (mt, a))
+            nc.vector.tensor_tensor(y[:], carried[mt, h][:, o : o + b - a], fresh[mt, a][:], ALU.subtract)
+            nc.sync.dma_start(out=out[mt * P : (mt + 1) * P, a:b], in_=y[:])
 
         cast("s", 0, 0, 1024)
         cast("v", 1, 0, 704)
@@ -218,44 +222,41 @@ def tile_picked_highway_tanh_l_kernel(tc, xT, res, w1, w2, offs, out):
         gather_x(0, 0, S)
         cast("s", 2, 0, 1024)
         cast("v", 3, 0, 512)
-        cast("v", 4, 0, 320)
-        cast("s", 4, 320, 512)
+        cast("v", 4, 0, 352)
+        cast("s", 4, 352, 512)
         gather_x(1, 0, 256)
         weave("s", 0, 256)
-        group_w(0)
         gather_x(1, 256, 512)
         weave("s", 256, 512)
-        gather_x(1, 512, 768)
-        weave("s", 512, 768)
-        gather_x(1, 768, 1024)
-        group_w(1)
-        weave("v", 768, 1024)
-        quantize_w(0)
+        gather_x(1, 512, 1024)
+        group_w(0)
+        weave("s", 512, 1024)
         quantize_x(0)
-        quantize_x(1)
-        quantize_w(1)
-        look_up(0)
+        quantize_w(0)
         look_up(1)
+        quantize_x(1)
+        by_feature(0, 0, 0, ACT.Sigmoid, -1.0)
+        group_w(1)
+        carry(0, 0)
+        quantize_w(1)
         by_feature(0, 1, 0, ACT.Sigmoid, -1.0)
-        by_feature(0, 1, 1, ACT.Sigmoid, -1.0)
-        by_feature(1, 0, 0, ACT.Tanh, -1.0)
-        by_token(0)
-        turn_passed(0)
-        by_feature(1, 0, 1, ACT.Tanh, -1.0)
         by_token(1)
+        by_feature(0, 1, 1, ACT.Sigmoid, -1.0)
         turn_passed(1)
-        carry(0, 512)
-        carry(512, 1024)
-        difference(0)
+        carry(1, 0)
+        carry(1, 1)
+        by_feature(1, 0, 1, ACT.Tanh, -1.0)
         difference(1)
+        by_feature(1, 0, 0, ACT.Tanh, 1.0)
         by_feature(1, 1, 0, ACT.Tanh, 1.0)
         by_feature(1, 1, 1, ACT.Tanh, 1.0)
-        weigh(0)
+        gate(0, 0, 512)
         weigh(1)
-        finish_low(0)
         finish_low(1)
-        gate(0)
-        gate(1)
-        finish_high(0, 512)
-        finish_high(512, 768)
-        finish_high(768, 1024)
+        finish(0, 0, 512)
+        gate(1, 0, 512)
+        gate(1, 512, 768)
+        finish(1, 0, 512)
+        gate(1, 768, 1024)
+        finish(1, 512, 768)
+        finish(1, 768, 1024)

@@ -72,7 +72,7 @@ def tile_picked_highway_tanh_l_kernel(tc, xT, res, w1, w2, offs, out):
         words = [pairs[u][:].rearrange("p t j -> p (t j)").bitcast(U32) for u in range(2)]
         picked = keep.tile([P, 2, S], U32, name="picked")
         woven = {}
-        x_codes = [keep.tile([P, HALF], U32, name="x_codes%d" % h, align_bytes=64) for h in range(2)]
+        x_codes = [keep.tile([P, HALF], U32, name="x_codes%d" % h, tag="x_codes%d" % h, align_bytes=64) for h in range(2)]
         x_scales = [keep.tile([P, HALF], U8, name="x_scales%d" % h, align_bytes=64) for h in range(2)]
 
         def gather_x(u, a, b):
@@ -99,7 +99,7 @@ def tile_picked_highway_tanh_l_kernel(tc, xT, res, w1, w2, offs, out):
                 in_=woven[h][:].rearrange("p n j -> p (n j)"),
             )
 
-        w_grouped = [keep.tile([P, N, PACK], BF16, name="w_grouped%d" % i, align_bytes=64) for i in range(2)]
+        w_grouped = [keep.tile([P, N, PACK], BF16, name="w_grouped%d" % i, tag="w_grouped%d" % i, align_bytes=64) for i in range(2)]
         w_codes = [keep.tile([P, N], U32, name="w_codes%d" % i, align_bytes=64) for i in range(2)]
         w_scales = [keep.tile([P, N], U8, name="w_scales%d" % i, align_bytes=64) for i in range(2)]
 
@@ -116,7 +116,7 @@ def tile_picked_highway_tanh_l_kernel(tc, xT, res, w1, w2, offs, out):
         vals = {}
 
         def by_feature(i, mt, h, func, scale):
-            acc = psum.tile([P, HALF], F32, name="acc", tag="acc")
+            acc = psum.tile([P, HALF], F32, name="acc", tag="acc", bufs=3)
             nc.tensor.matmul_mx(
                 out=acc[:],
                 lhsT=w_codes[i][:, mt * P : (mt + 1) * P].bitcast(FP8X4),
@@ -126,12 +126,18 @@ def tile_picked_highway_tanh_l_kernel(tc, xT, res, w1, w2, offs, out):
                 start=True,
                 stop=True,
             )
-            v = keep.tile([P, HALF], F32, name="val%d%d%d" % (i, mt, h))
-            nc.scalar.activation(v[:], acc[:], func, scale=scale)
+            if (i, mt, h) == (0, 1, 0):
+                vals["late"] = keep.tile([P, 2, HALF], F32, name="late", tag="w_raw1", align_bytes=64)
+                v = vals["late"][:, 0, :]
+            else:
+                tag = {(0, 1, 1): "w_grouped1"}.get((i, mt, h), "val%d%d%d" % (i, mt, h))
+                whole = keep.tile([P, HALF], F32, name="val%d%d%d" % (i, mt, h), tag=tag, align_bytes=64)
+                v = whole[:]
+            nc.scalar.activation(v, acc[:], func, scale=scale)
             vals[i, mt, h] = v
 
         def by_token(h):
-            acc = psum.tile([P, HALF], F32, name="acc", tag="acc")
+            acc = psum.tile([P, HALF], F32, name="acc", tag="acc", bufs=3)
             for t in range(BLOCKS):
                 cols = slice(t * P, (t + 1) * P)
                 nc.tensor.matmul_mx(
@@ -166,8 +172,8 @@ def tile_picked_highway_tanh_l_kernel(tc, xT, res, w1, w2, offs, out):
             passed[h] = r
 
         def turn_passed(h):
-            rt = keep.tile([P, HALF], F32, name="passed_t%d" % h)
-            nc.scalar.copy(out=rt[:], in_=turn([passed[h]])[:])
+            rt = vals["late"][:, 1, :]
+            nc.scalar.copy(out=rt, in_=turn([passed[h]])[:])
             passed_t[h] = rt
 
         diff = {}
@@ -197,7 +203,7 @@ def tile_picked_highway_tanh_l_kernel(tc, xT, res, w1, w2, offs, out):
         def carry(mt, h):
             q = keep.tile([P, HALF], F32, name="carried%d%d" % (mt, h))
             nc.vector.tensor_tensor(
-                q[:], res_rows[mt][:].indirect(entries(h * HALF, (h + 1) * HALF)), vals[0, mt, h][:], ALU.mult
+                q[:], res_rows[mt][:].indirect(entries(h * HALF, (h + 1) * HALF)), vals[0, mt, h], ALU.mult
             )
             carried[mt, h] = q
 
@@ -240,20 +246,20 @@ def tile_picked_highway_tanh_l_kernel(tc, xT, res, w1, w2, offs, out):
         carry(0, 0)
         quantize_w(1)
         by_feature(0, 1, 0, ACT.Sigmoid, -1.0)
-        by_token(1)
-        by_feature(0, 1, 1, ACT.Sigmoid, -1.0)
         turn_passed(1)
+        by_feature(0, 1, 1, ACT.Sigmoid, -1.0)
         carry(1, 0)
         carry(1, 1)
         by_feature(1, 0, 1, ACT.Tanh, -1.0)
+        by_token(1)
         difference(1)
         by_feature(1, 0, 0, ACT.Tanh, 1.0)
         by_feature(1, 1, 0, ACT.Tanh, 1.0)
         by_feature(1, 1, 1, ACT.Tanh, 1.0)
         gate(0, 0, 512)
         weigh(1)
-        finish_low(1)
         finish(0, 0, 512)
+        finish_low(1)
         gate(1, 0, 512)
         gate(1, 512, 768)
         finish(1, 0, 512)

@@ -19,7 +19,6 @@ ALU = mybir.AluOpType
 P = 128
 PACK = 4
 LIST_ROWS = 16
-CHUNK = 256
 HALF = 512
 BLOCKS = HALF // P
 
@@ -30,20 +29,17 @@ def tile_picked_highway_tanh_l_kernel(tc, xT, res, w1, w2, offs, out):
 
     with ExitStack() as ctx:
         keep = ctx.enter_context(tc.tile_pool(name="keep", bufs=1))
-        psum = ctx.enter_context(tc.psum_pool(name="psum", bufs=4))
+        psum = ctx.enter_context(tc.psum_pool(name="psum", bufs=1))
 
         offsets = keep.tile([P, S // LIST_ROWS], U16, name="offsets")
 
         def entries(a, b):
             return offsets[:, a // LIST_ROWS : b // LIST_ROWS]
 
-        warm_in = keep.tile([P, 8], F32, name="warm_in")
-        warm_out = keep.tile([P, 8], F32, name="warm_out")
-        nc.vector.memset(warm_in[:], 0.0)
-        nc.scalar.activation(warm_out[:], warm_in[:], ACT.Sigmoid)
         ident = keep.tile([P, P], F32, name="ident")
         make_identity(nc, ident[:])
 
+        res_rows = [keep.tile([P, T], F32, name="res%d" % mt) for mt in range(2)]
         x_loads = [(0, 0, 1024), (0, 1024, 2048), (1, 0, 1024), (1, 1024, 1536), (1, 1536, 2048)]
         x_raw = []
         for i, (u, a, b) in enumerate(x_loads):
@@ -52,9 +48,8 @@ def tile_picked_highway_tanh_l_kernel(tc, xT, res, w1, w2, offs, out):
             x_raw.append(raw)
             if i == 0:
                 nc.sync.dma_start(offsets[:], offs)
-        res_rows = [keep.tile([P, T], F32, name="res%d" % mt, tag="res%d" % mt) for mt in range(2)]
         w_raw = [keep.tile([P, PACK, N], F32, name="w_raw%d" % i, tag="w_raw%d" % i, align_bytes=64) for i in range(2)]
-        for i, w in enumerate((w2, w1)):
+        for i, w in enumerate((w1, w2)):
             nc.sync.dma_start(out=w_raw[i][:], in_=w.rearrange("(p j) n -> p j n", j=PACK))
             nc.sync.dma_start(out=res_rows[i][:], in_=res[i * P : (i + 1) * P, :])
 
@@ -70,53 +65,50 @@ def tile_picked_highway_tanh_l_kernel(tc, xT, res, w1, w2, offs, out):
                 nc.scalar.copy(out=dst, in_=src)
 
         words = [pairs[u][:].rearrange("p t j -> p (t j)").bitcast(U32) for u in range(2)]
-        picked = keep.tile([P, 2, S], U32, name="picked")
-        woven = {}
-        x_codes = [keep.tile([P, HALF], U32, name="x_codes%d" % h, tag="x_codes%d" % h, align_bytes=64) for h in range(2)]
+        picked = [keep.tile([P, 2, HALF], U32, name="picked%d" % h, tag="picked%d" % h, align_bytes=64) for h in range(2)]
+        woven = []
+        x_codes = [keep.tile([P, HALF], U32, name="x_codes%d" % h, align_bytes=64) for h in range(2)]
         x_scales = [keep.tile([P, HALF], U8, name="x_scales%d" % h, align_bytes=64) for h in range(2)]
 
-        def gather_x(u, a, b):
-            nc.vector.tensor_copy(out=picked[:, u, a:b], in_=words[u].indirect(entries(a, b)))
+        def gather_x(u, h):
+            nc.vector.tensor_copy(out=picked[h][:, u, :], in_=words[u].indirect(entries(h * HALF, (h + 1) * HALF)))
 
-        def weave(engine, a, b):
-            h, o = divmod(a, HALF)
-            if o == 0:
-                woven[h] = keep.tile([P, HALF, PACK], BF16, name="woven%d" % h, tag=("woven0", "w_raw0")[h], align_bytes=64)
-            dst = woven[h][:].rearrange("p n j -> p (n j)").bitcast(U32).rearrange("p (n u) -> p n u", u=2)
-            src = picked[:, :, a:b].rearrange("p u n -> p n u")
-            if engine == "v":
-                flat = woven[h][:].rearrange("p n j -> p (n j)").bitcast(I32).rearrange("p (n u) -> p n u", u=2)
-                nc.vector.tensor_copy(
-                    out=flat[:, o : o + b - a, :], in_=picked[:].bitcast(I32)[:, :, a:b].rearrange("p u n -> p n u")
-                )
-            else:
-                nc.scalar.copy(out=dst[:, o : o + b - a, :], in_=src)
+        def weave(h):
+            if h == 0:
+                woven.append(keep.tile([P, S * PACK], BF16, name="woven", tag="w_raw0", align_bytes=64))
+            dst = woven[0][:].bitcast(U32).rearrange("p (n u) -> p n u", u=2)
+            nc.scalar.copy(out=dst[:, h * HALF : (h + 1) * HALF, :], in_=picked[h][:].rearrange("p u n -> p n u"))
 
         def quantize_x(h):
             nc.vector.quantize_mx(
                 out=x_codes[h][:].bitcast(FP8X4),
                 scales=x_scales[h][:],
-                in_=woven[h][:].rearrange("p n j -> p (n j)"),
+                in_=woven[0][:, h * HALF * PACK : (h + 1) * HALF * PACK],
             )
 
-        w_grouped = [keep.tile([P, N, PACK], BF16, name="w_grouped%d" % i, tag="w_grouped%d" % i, align_bytes=64) for i in range(2)]
+        w_grouped = {}
         w_codes = [keep.tile([P, N], U32, name="w_codes%d" % i, align_bytes=64) for i in range(2)]
         w_scales = [keep.tile([P, N], U8, name="w_scales%d" % i, align_bytes=64) for i in range(2)]
 
         def group_w(i):
-            nc.scalar.copy(out=w_grouped[i][:], in_=w_raw[i][:].rearrange("p t c -> p c t"))
+            whole = keep.tile([P, N * PACK], BF16, name="w_grouped%d" % i, tag="w_grouped", align_bytes=64)
+            w_grouped[i] = whole[:]
+            nc.scalar.copy(
+                out=w_grouped[i].rearrange("p (c i t) -> p c t i", i=4, t=PACK),
+                in_=w_raw[i][:].rearrange("p t (c i) -> p c t i", i=4),
+            )
 
         def quantize_w(i):
             nc.vector.quantize_mx(
                 out=w_codes[i][:].bitcast(FP8X4),
                 scales=w_scales[i][:],
-                in_=w_grouped[i][:].rearrange("p n j -> p (n j)"),
+                in_=w_grouped[i],
             )
 
         vals = {}
 
-        def by_feature(i, mt, h, func, scale):
-            acc = psum.tile([P, HALF], F32, name="acc", tag="acc", bufs=3)
+        def by_feature(i, mt, h, scale):
+            acc = psum.tile([P, HALF], F32, name="acc", tag="acc", bufs=4)
             nc.tensor.matmul_mx(
                 out=acc[:],
                 lhsT=w_codes[i][:, mt * P : (mt + 1) * P].bitcast(FP8X4),
@@ -126,143 +118,133 @@ def tile_picked_highway_tanh_l_kernel(tc, xT, res, w1, w2, offs, out):
                 start=True,
                 stop=True,
             )
-            if (i, mt, h) == (0, 1, 0):
-                vals["late"] = keep.tile([P, 2, HALF], F32, name="late", tag="w_raw1", align_bytes=64)
-                v = vals["late"][:, 0, :]
-            else:
-                tag = {(0, 1, 1): "w_grouped1"}.get((i, mt, h), "val%d%d%d" % (i, mt, h))
-                whole = keep.tile([P, HALF], F32, name="val%d%d%d" % (i, mt, h), tag=tag, align_bytes=64)
-                v = whole[:]
-            nc.scalar.activation(v, acc[:], func, scale=scale)
+            v = keep.tile([P, HALF], F32, name="val%d%d%d" % (i, mt, h))
+            nc.scalar.activation(v[:], acc[:], ACT.Tanh, scale=scale)
             vals[i, mt, h] = v
 
         def by_token(h):
-            acc = psum.tile([P, HALF], F32, name="acc", tag="acc", bufs=3)
+            acc = psum.tile([P, HALF], F32, name="acc", tag="acc", bufs=4)
             for t in range(BLOCKS):
                 cols = slice(t * P, (t + 1) * P)
                 nc.tensor.matmul_mx(
                     out=acc[:, cols],
                     lhsT=x_codes[h][:, cols].bitcast(FP8X4),
                     lhsT_scale=x_scales[h][:, cols],
-                    rhs=w_codes[0][:, 0:P].bitcast(FP8X4),
-                    rhs_scale=w_scales[0][:, 0:P],
+                    rhs=w_codes[1][:, 0:P].bitcast(FP8X4),
+                    rhs_scale=w_scales[1][:, 0:P],
                     start=True,
                     stop=True,
                 )
             v = keep.tile([P, HALF], F32, name="gate_t%d" % h)
-            nc.scalar.activation(v[:], acc[:], ACT.Sigmoid)
-            vals[0, 0, h] = v
+            nc.scalar.activation(v[:], acc[:], ACT.Tanh, scale=0.5)
+            vals[1, 0, h] = v
 
-        def turn(sources):
-            bank = psum.tile([P, HALF], F32, name="turned", tag="turned")
-            for n, src in enumerate(sources):
-                for t in range(BLOCKS):
-                    cols = slice(t * P, (t + 1) * P)
-                    nc.tensor.matmul(
-                        bank[:, cols], src[:, cols], ident[:], is_transpose=True,
-                        start=(n == 0 and t == 0), stop=(n == len(sources) - 1 and t == BLOCKS - 1),
-                    )
-            return bank
+        def turn(bank, src, first, last):
+            for t in range(BLOCKS):
+                cols = slice(t * P, (t + 1) * P)
+                nc.tensor.matmul(
+                    bank[:, cols], src[:, cols], ident[:], is_transpose=True,
+                    start=(first and t == 0), stop=(last and t == BLOCKS - 1),
+                )
 
-        passed, passed_t, pull = {}, {}, {}
+        diff, total, pull = {}, {}, {}
+
+        passed = {}
 
         def look_up(h):
-            r = keep.tile([P, HALF], F32, name="passed%d" % h)
-            nc.vector.tensor_copy(out=r[:], in_=res_rows[0][:].indirect(entries(h * HALF, (h + 1) * HALF)))
-            passed[h] = r
+            whole = keep.tile([P, HALF], F32, name="passed%d" % h, tag="picked0", align_bytes=64)
+            passed[h] = whole[:]
+            nc.vector.tensor_copy(out=passed[h], in_=res_rows[0][:].indirect(entries(h * HALF, (h + 1) * HALF)))
 
         def turn_passed(h):
-            rt = vals["late"][:, 1, :]
-            nc.scalar.copy(out=rt, in_=turn([passed[h]])[:])
-            passed_t[h] = rt
-
-        diff = {}
+            turned = psum.tile([P, HALF], F32, name="turned%d" % h, tag="total%d" % h)
+            turn(turned, passed[h], True, True)
+            rt = keep.tile([P, HALF], F32, name="passed_t%d" % h)
+            nc.scalar.activation(rt[:], turned[:], ACT.Copy, scale=-2.0)
+            total[h] = psum.tile([P, HALF], F32, name="total%d" % h, tag="total%d" % h)
+            turn(total[h], rt, True, False)
 
         def difference(h):
-            diff[h] = turn([passed[h], vals[1, 0, h]])
+            diff[h] = psum.tile([P, HALF], F32, name="diff%d" % h, tag="diff%d" % h)
+            turn(diff[h], passed[h], True, False)
+            turn(diff[h], vals[0, 0, h], False, True)
 
         def weigh(h):
-            d = diff[h]
-            e_tile = keep.tile([P, HALF], F32, name="pull%d" % h)
-            e = e_tile[:]
-            nc.vector.scalar_tensor_tensor(out=e, in0=d[:], scalar=-1.0, in1=vals[0, 0, h][:], op0=ALU.mult, op1=ALU.mult)
-            pull[h] = e
+            e = keep.tile([P, HALF], F32, name="pull%d" % h)
+            nc.vector.scalar_tensor_tensor(out=e[:], in0=vals[1, 0, h][:], scalar=1.0, in1=diff[h][:], op0=ALU.add, op1=ALU.mult)
+            turn(total[h], e, False, True)
 
         def finish_low(h):
             y = keep.tile([P, HALF], F32, name="low%d" % h)
-            nc.scalar.copy(out=y[:], in_=turn([passed_t[h], pull[h]])[:])
+            nc.scalar.activation(y[:], total[h][:], ACT.Copy, scale=-0.5)
             nc.sync.dma_start(out=out[0:P, h * HALF : (h + 1) * HALF], in_=y[:])
 
-        def finish_low_v(h):
-            y = keep.tile([P, HALF], F32, name="low%d" % h)
-            nc.vector.tensor_tensor(y[:], turn([pull[h]])[:], passed[h][:], ALU.add)
-            nc.sync.dma_start(out=out[0:P, h * HALF : (h + 1) * HALF], in_=y[:])
-
-        carried, fresh = {}, {}
+        gap, part = {}, {}
 
         def carry(mt, h):
-            q = keep.tile([P, HALF], F32, name="carried%d%d" % (mt, h))
+            q = keep.tile([P, HALF], F32, name="gap%d%d" % (mt, h))
             nc.vector.tensor_tensor(
-                q[:], res_rows[mt][:].indirect(entries(h * HALF, (h + 1) * HALF)), vals[0, mt, h], ALU.mult
+                q[:], res_rows[mt][:].indirect(entries(h * HALF, (h + 1) * HALF)), vals[0, mt, h][:], ALU.subtract
             )
-            carried[mt, h] = q
+            gap[mt, h] = q
 
         def gate(mt, a, b):
             h, o = divmod(a, HALF)
             cols = slice(o, o + b - a)
-            g = keep.tile([P, b - a], F32, name="fresh%d_%d" % (mt, a))
+            g = keep.tile([P, b - a], F32, name="part%d_%d" % (mt, a))
             nc.vector.scalar_tensor_tensor(
-                out=g[:], in0=vals[0, mt, h][:, cols], scalar=-1.0, in1=vals[1, mt, h][:, cols], op0=ALU.add, op1=ALU.mult
+                out=g[:], in0=vals[1, mt, h][:, cols], scalar=-1.0, in1=gap[mt, h][:, cols], op0=ALU.add, op1=ALU.mult
             )
-            fresh[mt, a] = g
+            part[mt, a] = g
 
         def finish(mt, a, b):
             h, o = divmod(a, HALF)
             y = keep.tile([P, b - a], F32, name="result%d_%d" % (mt, a))
-            nc.vector.tensor_tensor(y[:], carried[mt, h][:, o : o + b - a], fresh[mt, a][:], ALU.subtract)
+            nc.vector.scalar_tensor_tensor(
+                out=y[:], in0=part[mt, a][:], scalar=-0.5, in1=vals[0, mt, h][:, o : o + b - a], op0=ALU.mult, op1=ALU.add
+            )
             nc.sync.dma_start(out=out[mt * P : (mt + 1) * P, a:b], in_=y[:])
 
         cast("s", 0, 0, 1024)
         cast("v", 1, 0, 704)
         cast("s", 1, 704, 1024)
-        gather_x(0, 0, S)
+        gather_x(0, 0)
+        gather_x(0, 1)
         cast("s", 2, 0, 1024)
         cast("v", 3, 0, 512)
         cast("v", 4, 0, 352)
         cast("s", 4, 352, 512)
-        gather_x(1, 0, 256)
-        weave("s", 0, 256)
-        gather_x(1, 256, 512)
-        weave("s", 256, 512)
-        gather_x(1, 512, 1024)
+        gather_x(1, 0)
+        gather_x(1, 1)
         group_w(0)
-        weave("s", 512, 1024)
-        quantize_x(0)
+        weave(0)
+        weave(1)
         quantize_w(0)
-        look_up(1)
-        quantize_x(1)
-        by_feature(0, 0, 0, ACT.Sigmoid, -1.0)
+        quantize_x(0)
         group_w(1)
-        carry(0, 0)
+        look_up(1)
+        by_feature(0, 0, 0, 1.0)
+        by_feature(0, 1, 0, 1.0)
+        quantize_x(1)
         quantize_w(1)
-        by_feature(0, 1, 0, ACT.Sigmoid, -1.0)
         turn_passed(1)
-        by_feature(0, 1, 1, ACT.Sigmoid, -1.0)
-        carry(1, 0)
-        carry(1, 1)
-        by_feature(1, 0, 1, ACT.Tanh, -1.0)
+        by_feature(0, 0, 1, -1.0)
+        carry(0, 0)
+        by_feature(1, 0, 0, 0.5)
         by_token(1)
         difference(1)
-        by_feature(1, 0, 0, ACT.Tanh, 1.0)
-        by_feature(1, 1, 0, ACT.Tanh, 1.0)
-        by_feature(1, 1, 1, ACT.Tanh, 1.0)
+        carry(1, 0)
+        by_feature(1, 1, 0, 0.5)
+        by_feature(0, 1, 1, 1.0)
         gate(0, 0, 512)
         weigh(1)
+        by_feature(1, 1, 1, 0.5)
         finish(0, 0, 512)
         finish_low(1)
         gate(1, 0, 512)
-        gate(1, 512, 768)
+        carry(1, 1)
         finish(1, 0, 512)
+        gate(1, 512, 768)
         gate(1, 768, 1024)
         finish(1, 512, 768)
         finish(1, 768, 1024)

@@ -40,7 +40,7 @@ def tile_picked_highway_tanh_l_kernel(tc, xT, res, w1, w2, offs, out):
         make_identity(nc, ident[:])
 
         res_rows = [keep.tile([P, T], F32, name="res%d" % mt) for mt in range(2)]
-        x_loads = [(0, 0, 1024), (0, 1024, 2048), (1, 0, 1024), (1, 1024, 1536), (1, 1536, 2048)]
+        x_loads = [(0, 0, 1024), (0, 1024, 2048), (1, 0, 1024), (1, 1024, 1664), (1, 1664, 2048)]
         x_raw = []
         for i, (u, a, b) in enumerate(x_loads):
             raw = keep.tile([P, 2, b - a], F32, name="x_raw%d" % i)
@@ -73,11 +73,16 @@ def tile_picked_highway_tanh_l_kernel(tc, xT, res, w1, w2, offs, out):
         def gather_x(u, h):
             nc.vector.tensor_copy(out=picked[h][:, u, :], in_=words[u].indirect(entries(h * HALF, (h + 1) * HALF)))
 
-        def weave(h):
-            if h == 0:
+        def weave(engine, h, a, b):
+            if not woven:
                 woven.append(keep.tile([P, S * PACK], BF16, name="woven", tag="w_raw0", align_bytes=64))
-            dst = woven[0][:].bitcast(U32).rearrange("p (n u) -> p n u", u=2)
-            nc.scalar.copy(out=dst[:, h * HALF : (h + 1) * HALF, :], in_=picked[h][:].rearrange("p u n -> p n u"))
+            word = I32 if engine == "v" else U32
+            dst = woven[0][:].bitcast(word).rearrange("p (n u) -> p n u", u=2)[:, h * HALF + a : h * HALF + b, :]
+            src = picked[h][:].bitcast(word)[:, :, a:b].rearrange("p u n -> p n u")
+            if engine == "v":
+                nc.vector.tensor_copy(out=dst, in_=src)
+            else:
+                nc.scalar.copy(out=dst, in_=src)
 
         def quantize_x(h):
             nc.vector.quantize_mx(
@@ -108,7 +113,10 @@ def tile_picked_highway_tanh_l_kernel(tc, xT, res, w1, w2, offs, out):
         vals = {}
 
         def by_feature(i, mt, h, scale):
-            acc = psum.tile([P, HALF], F32, name="acc", tag="acc", bufs=4)
+            if (i, mt, h) == (0, 0, 1):
+                acc = psum.tile([P, HALF], F32, name="acc_low", tag="total")
+            else:
+                acc = psum.tile([P, HALF], F32, name="acc", tag="acc", bufs=4)
             nc.tensor.matmul_mx(
                 out=acc[:],
                 lhsT=w_codes[i][:, mt * P : (mt + 1) * P].bitcast(FP8X4),
@@ -118,8 +126,15 @@ def tile_picked_highway_tanh_l_kernel(tc, xT, res, w1, w2, offs, out):
                 start=True,
                 stop=True,
             )
-            v = keep.tile([P, HALF], F32, name="val%d%d%d" % (i, mt, h))
-            nc.scalar.activation(v[:], acc[:], ACT.Tanh, scale=scale)
+            if i == 0 and (mt, h) != (1, 1):
+                if (mt, h) == (0, 0):
+                    vals["first"] = keep.tile([P, 4 * HALF], F32, name="first", tag="w_raw1", align_bytes=64)
+                slot = mt + 2 * h
+                v = vals["first"][:, slot * HALF : (slot + 1) * HALF]
+            else:
+                whole = keep.tile([P, HALF], F32, name="val%d%d%d" % (i, mt, h))
+                v = whole[:]
+            nc.scalar.activation(v, acc[:], ACT.Tanh, scale=scale)
             vals[i, mt, h] = v
 
         def by_token(h):
@@ -156,22 +171,25 @@ def tile_picked_highway_tanh_l_kernel(tc, xT, res, w1, w2, offs, out):
             passed[h] = whole[:]
             nc.vector.tensor_copy(out=passed[h], in_=res_rows[0][:].indirect(entries(h * HALF, (h + 1) * HALF)))
 
+        passed_t = {}
+
         def turn_passed(h):
-            turned = psum.tile([P, HALF], F32, name="turned%d" % h, tag="total%d" % h)
+            turned = psum.tile([P, HALF], F32, name="turned", tag="diff")
             turn(turned, passed[h], True, True)
-            rt = keep.tile([P, HALF], F32, name="passed_t%d" % h)
-            nc.scalar.activation(rt[:], turned[:], ACT.Copy, scale=-2.0)
-            total[h] = psum.tile([P, HALF], F32, name="total%d" % h, tag="total%d" % h)
-            turn(total[h], rt, True, False)
+            rt = vals["first"][:, 3 * HALF : 4 * HALF]
+            nc.scalar.activation(rt, turned[:], ACT.Copy, scale=-2.0)
+            passed_t[h] = rt
 
         def difference(h):
-            diff[h] = psum.tile([P, HALF], F32, name="diff%d" % h, tag="diff%d" % h)
+            diff[h] = psum.tile([P, HALF], F32, name="diff", tag="diff")
             turn(diff[h], passed[h], True, False)
             turn(diff[h], vals[0, 0, h], False, True)
 
         def weigh(h):
             e = keep.tile([P, HALF], F32, name="pull%d" % h)
             nc.vector.scalar_tensor_tensor(out=e[:], in0=vals[1, 0, h][:], scalar=1.0, in1=diff[h][:], op0=ALU.add, op1=ALU.mult)
+            total[h] = psum.tile([P, HALF], F32, name="total", tag="total")
+            turn(total[h], passed_t[h], True, False)
             turn(total[h], e, False, True)
 
         def finish_low(h):
@@ -184,7 +202,7 @@ def tile_picked_highway_tanh_l_kernel(tc, xT, res, w1, w2, offs, out):
         def carry(mt, h):
             q = keep.tile([P, HALF], F32, name="gap%d%d" % (mt, h))
             nc.vector.tensor_tensor(
-                q[:], res_rows[mt][:].indirect(entries(h * HALF, (h + 1) * HALF)), vals[0, mt, h][:], ALU.subtract
+                q[:], res_rows[mt][:].indirect(entries(h * HALF, (h + 1) * HALF)), vals[0, mt, h], ALU.subtract
             )
             gap[mt, h] = q
 
@@ -211,14 +229,15 @@ def tile_picked_highway_tanh_l_kernel(tc, xT, res, w1, w2, offs, out):
         gather_x(0, 0)
         gather_x(0, 1)
         cast("s", 2, 0, 1024)
-        cast("v", 3, 0, 512)
-        cast("v", 4, 0, 352)
-        cast("s", 4, 352, 512)
+        cast("v", 3, 0, 640)
+        cast("v", 4, 0, 256)
+        cast("s", 4, 256, 384)
         gather_x(1, 0)
         gather_x(1, 1)
         group_w(0)
-        weave(0)
-        weave(1)
+        weave("s", 0, 0, 384)
+        weave("v", 0, 384, 512)
+        weave("s", 1, 0, 512)
         quantize_w(0)
         quantize_x(0)
         group_w(1)
@@ -244,7 +263,7 @@ def tile_picked_highway_tanh_l_kernel(tc, xT, res, w1, w2, offs, out):
         gate(1, 0, 512)
         carry(1, 1)
         finish(1, 0, 512)
-        gate(1, 512, 768)
-        gate(1, 768, 1024)
-        finish(1, 512, 768)
-        finish(1, 768, 1024)
+        gate(1, 512, 832)
+        gate(1, 832, 1024)
+        finish(1, 512, 832)
+        finish(1, 832, 1024)

@@ -40,7 +40,7 @@ def tile_picked_highway_tanh_l_kernel(tc, xT, res, w1, w2, offs, out):
         make_identity(nc, ident[:])
 
         res_rows = [keep.tile([P, T], F32, name="res%d" % mt) for mt in range(2)]
-        x_loads = [(0, 0, 1024), (0, 1024, 2048), (1, 0, 1024), (1, 1024, 1664), (1, 1664, 2048)]
+        x_loads = [(0, 0, 1024), (0, 1024, 2048), (1, 0, 768), (1, 768, 1664), (1, 1664, 2048)]
         x_raw = []
         for i, (u, a, b) in enumerate(x_loads):
             raw = keep.tile([P, 2, b - a], F32, name="x_raw%d" % i)
@@ -199,27 +199,31 @@ def tile_picked_highway_tanh_l_kernel(tc, xT, res, w1, w2, offs, out):
 
         gap, part = {}, {}
 
-        def carry(mt, h):
-            q = keep.tile([P, HALF], F32, name="gap%d%d" % (mt, h))
+        def carry(mt, a, b):
+            h, o = divmod(a, HALF)
+            if (mt, a) == (1, 704):
+                q = vals[1, 1, 0][:, 0 : b - a]
+            else:
+                q = keep.tile([P, b - a], F32, name="gap%d_%d" % (mt, a))
             nc.vector.tensor_tensor(
-                q[:], res_rows[mt][:].indirect(entries(h * HALF, (h + 1) * HALF)), vals[0, mt, h], ALU.subtract
+                q[:], res_rows[mt][:].indirect(entries(a, b)), vals[0, mt, h][:, o : o + b - a], ALU.subtract
             )
-            gap[mt, h] = q
+            gap[mt, a] = q
 
         def gate(mt, a, b):
             h, o = divmod(a, HALF)
             cols = slice(o, o + b - a)
             g = keep.tile([P, b - a], F32, name="part%d_%d" % (mt, a))
             nc.vector.scalar_tensor_tensor(
-                out=g[:], in0=vals[1, mt, h][:, cols], scalar=-1.0, in1=gap[mt, h][:, cols], op0=ALU.add, op1=ALU.mult
+                out=g[:], in0=vals[1, mt, h][:, cols], scalar=-1.0, in1=gap[mt, a][:], op0=ALU.add, op1=ALU.mult
             )
             part[mt, a] = g
 
-        def finish(mt, a, b):
+        def finish(mt, a, b, first):
             h, o = divmod(a, HALF)
             y = keep.tile([P, b - a], F32, name="result%d_%d" % (mt, a))
             nc.vector.scalar_tensor_tensor(
-                out=y[:], in0=part[mt, a][:], scalar=-0.5, in1=vals[0, mt, h][:, o : o + b - a], op0=ALU.mult, op1=ALU.add
+                out=y[:], in0=part[mt, first][:, a - first : b - first], scalar=-0.5, in1=vals[0, mt, h][:, o : o + b - a], op0=ALU.mult, op1=ALU.add
             )
             nc.sync.dma_start(out=out[mt * P : (mt + 1) * P, a:b], in_=y[:])
 
@@ -228,8 +232,9 @@ def tile_picked_highway_tanh_l_kernel(tc, xT, res, w1, w2, offs, out):
         cast("s", 1, 704, 1024)
         gather_x(0, 0)
         gather_x(0, 1)
-        cast("s", 2, 0, 1024)
-        cast("v", 3, 0, 640)
+        cast("s", 2, 0, 768)
+        cast("v", 3, 0, 576)
+        cast("s", 3, 576, 896)
         cast("v", 4, 0, 256)
         cast("s", 4, 256, 384)
         gather_x(1, 0)
@@ -248,22 +253,24 @@ def tile_picked_highway_tanh_l_kernel(tc, xT, res, w1, w2, offs, out):
         quantize_w(1)
         turn_passed(1)
         by_feature(0, 0, 1, -1.0)
-        carry(0, 0)
+        carry(0, 0, 512)
         by_feature(1, 0, 0, 0.5)
         by_token(1)
         difference(1)
-        carry(1, 0)
+        carry(1, 0, 512)
         by_feature(1, 1, 0, 0.5)
         by_feature(0, 1, 1, 1.0)
         gate(0, 0, 512)
         weigh(1)
         by_feature(1, 1, 1, 0.5)
-        finish(0, 0, 512)
+        finish(0, 0, 512, 0)
         finish_low(1)
         gate(1, 0, 512)
-        carry(1, 1)
-        finish(1, 0, 512)
-        gate(1, 512, 832)
-        gate(1, 832, 1024)
-        finish(1, 512, 832)
-        finish(1, 832, 1024)
+        carry(1, 512, 704)
+        finish(1, 0, 512, 0)
+        carry(1, 704, 1024)
+        gate(1, 512, 704)
+        gate(1, 704, 1024)
+        finish(1, 512, 704, 512)
+        finish(1, 704, 896, 704)
+        finish(1, 896, 1024, 704)

@@ -201,7 +201,7 @@ def tile_picked_highway_tanh_l_kernel(tc, xT, res, w1, w2, offs, out):
 
         def carry(mt, a, b):
             h, o = divmod(a, HALF)
-            if (mt, a) == (1, 704):
+            if (mt, a) == (1, 768):
                 q = vals[1, 1, 0][:, 0 : b - a]
             else:
                 q = keep.tile([P, b - a], F32, name="gap%d_%d" % (mt, a))
@@ -266,11 +266,11 @@ def tile_picked_highway_tanh_l_kernel(tc, xT, res, w1, w2, offs, out):
         finish(0, 0, 512, 0)
         finish_low(1)
         gate(1, 0, 512)
-        carry(1, 512, 704)
+        carry(1, 512, 768)
         finish(1, 0, 512, 0)
-        carry(1, 704, 1024)
-        gate(1, 512, 704)
-        gate(1, 704, 1024)
-        finish(1, 512, 704, 512)
-        finish(1, 704, 896, 704)
-        finish(1, 896, 1024, 704)
+        carry(1, 768, 1024)
+        gate(1, 512, 768)
+        gate(1, 768, 1024)
+        finish(1, 512, 768, 512)
+        finish(1, 768, 896, 768)
+        finish(1, 896, 1024, 768)

@@ -48,9 +48,12 @@ def tile_picked_highway_tanh_l_kernel(tc, xT, res, w1, w2, offs, out):
             x_raw.append(raw)
             if i == 0:
                 nc.sync.dma_start(offsets[:], offs)
-        w_raw = [keep.tile([P, PACK, N], F32, name="w_raw%d" % i, tag="w_raw%d" % i, align_bytes=64) for i in range(2)]
+        w_parts = [[(0, N)], [(0, P), (P, N)]]
+        w_raw = {}
         for i, w in enumerate((w1, w2)):
-            nc.sync.dma_start(out=w_raw[i][:], in_=w.rearrange("(p j) n -> p j n", j=PACK))
+            for a, b in w_parts[i]:
+                w_raw[i, a] = keep.tile([P, PACK, b - a], F32, name="w_raw%d_%d" % (i, a), tag="w_raw%d_%d" % (i, a), align_bytes=64)
+                nc.sync.dma_start(out=w_raw[i, a][:], in_=w.rearrange("(p j) n -> p j n", j=PACK)[:, :, a:b])
             nc.sync.dma_start(out=res_rows[i][:], in_=res[i * P : (i + 1) * P, :])
 
         pairs = [keep.tile([P, T, 2], BF16, name="pairs%d" % u) for u in range(2)]
@@ -75,7 +78,7 @@ def tile_picked_highway_tanh_l_kernel(tc, xT, res, w1, w2, offs, out):
 
         def weave(engine, h, a, b):
             if not woven:
-                woven.append(keep.tile([P, S * PACK], BF16, name="woven", tag="w_raw0", align_bytes=64))
+                woven.append(keep.tile([P, S * PACK], BF16, name="woven", tag="w_raw0_0", align_bytes=64))
             word = I32 if engine == "v" else U32
             dst = woven[0][:].bitcast(word).rearrange("p (n u) -> p n u", u=2)[:, h * HALF + a : h * HALF + b, :]
             src = picked[h][:].bitcast(word)[:, :, a:b].rearrange("p u n -> p n u")
@@ -98,10 +101,11 @@ def tile_picked_highway_tanh_l_kernel(tc, xT, res, w1, w2, offs, out):
         def group_w(i):
             whole = keep.tile([P, N * PACK], BF16, name="w_grouped%d" % i, tag="w_grouped", align_bytes=64)
             w_grouped[i] = whole[:]
-            nc.scalar.copy(
-                out=w_grouped[i].rearrange("p (c i t) -> p c t i", i=4, t=PACK),
-                in_=w_raw[i][:].rearrange("p t (c i) -> p c t i", i=4),
-            )
+            for a, b in w_parts[i]:
+                nc.scalar.copy(
+                    out=w_grouped[i][:, a * PACK : b * PACK].rearrange("p (c i t) -> p c t i", i=4, t=PACK),
+                    in_=w_raw[i, a][:].rearrange("p t (c i) -> p c t i", i=4),
+                )
 
         def quantize_w(i):
             nc.vector.quantize_mx(
@@ -128,7 +132,7 @@ def tile_picked_highway_tanh_l_kernel(tc, xT, res, w1, w2, offs, out):
             )
             if i == 0 and (mt, h) != (1, 1):
                 if (mt, h) == (0, 0):
-                    vals["first"] = keep.tile([P, 4 * HALF], F32, name="first", tag="w_raw1", align_bytes=64)
+                    vals["first"] = keep.tile([P, 4 * HALF], F32, name="first", tag="w_raw1_0", align_bytes=64)
                 slot = mt + 2 * h
                 v = vals["first"][:, slot * HALF : (slot + 1) * HALF]
             else:
@@ -272,5 +276,4 @@ def tile_picked_highway_tanh_l_kernel(tc, xT, res, w1, w2, offs, out):
         gate(1, 512, 768)
         gate(1, 768, 1024)
         finish(1, 512, 768, 512)
-        finish(1, 768, 896, 768)
-        finish(1, 896, 1024, 768)
+        finish(1, 768, 1024, 768)

@@ -9,7 +9,6 @@ FLOPS = 2 * 2 * K * N * S
 F32 = mybir.dt.float32
 BF16 = mybir.dt.bfloat16
 U32 = mybir.dt.uint32
-I32 = mybir.dt.int32
 U16 = mybir.dt.uint16
 U8 = mybir.dt.uint8
 FP8X4 = mybir.dt.float8_e4m3fn_x4
@@ -20,7 +19,14 @@ P = 128
 PACK = 4
 LIST_ROWS = 16
 HALF = 512
-BLOCKS = HALF // P
+PIECE = 256
+ACC_BANKS = 4
+LAYER, GATE = 0, 1
+
+X_LOADS = [(0, 0, 1024), (0, 1024, 2048), (1, 0, 768), (1, 768, 1664), (1, 1664, 2048)]
+VECTOR_COLUMNS = [0, 704, 0, 576, 256]
+W_PARTS = [[(0, N)], [(0, P), (P, N)]]
+LEAD = PIECE
 
 
 def tile_picked_highway_tanh_l_kernel(tc, xT, res, w1, w2, offs, out):
@@ -40,87 +46,76 @@ def tile_picked_highway_tanh_l_kernel(tc, xT, res, w1, w2, offs, out):
         make_identity(nc, ident[:])
 
         res_rows = [keep.tile([P, T], F32, name="res%d" % mt) for mt in range(2)]
-        x_loads = [(0, 0, 1024), (0, 1024, 2048), (1, 0, 768), (1, 768, 1664), (1, 1664, 2048)]
         x_raw = []
-        for i, (u, a, b) in enumerate(x_loads):
+        for i, (u, a, b) in enumerate(X_LOADS):
             raw = keep.tile([P, 2, b - a], F32, name="x_raw%d" % i)
             nc.sync.dma_start(out=raw[:], in_=x_rows[:, 2 * u : 2 * u + 2, a:b])
             x_raw.append(raw)
             if i == 0:
                 nc.sync.dma_start(offsets[:], offs)
-        w_parts = [[(0, N)], [(0, P), (P, N)]]
         w_raw = {}
         for i, w in enumerate((w1, w2)):
-            for a, b in w_parts[i]:
-                w_raw[i, a] = keep.tile([P, PACK, b - a], F32, name="w_raw%d_%d" % (i, a), tag="w_raw%d_%d" % (i, a), align_bytes=64)
+            for a, b in W_PARTS[i]:
+                w_raw[i, a] = keep.tile(
+                    [P, PACK, b - a], F32, name="w_raw%d_%d" % (i, a), tag="w_raw%d_%d" % (i, a), align_bytes=64
+                )
                 nc.sync.dma_start(out=w_raw[i, a][:], in_=w.rearrange("(p j) n -> p j n", j=PACK)[:, :, a:b])
             nc.sync.dma_start(out=res_rows[i][:], in_=res[i * P : (i + 1) * P, :])
 
         pairs = [keep.tile([P, T, 2], BF16, name="pairs%d" % u) for u in range(2)]
 
-        def cast(engine, i, a, b):
-            u, a0, b0 = x_loads[i]
-            src = x_raw[i][:, :, a:b].rearrange("p j c -> p c j")
-            dst = pairs[u][:, a0 + a : a0 + b, :]
-            if engine == "v":
-                nc.vector.tensor_copy(out=dst, in_=src)
-            else:
-                nc.scalar.copy(out=dst, in_=src)
+        def round_load(i):
+            u, a, b = X_LOADS[i]
+            src = x_raw[i][:].rearrange("p j c -> p c j")
+            dst = pairs[u][:, a:b, :]
+            split = VECTOR_COLUMNS[i]
+            if split:
+                nc.vector.tensor_copy(out=dst[:, 0:split, :], in_=src[:, 0:split, :])
+            nc.scalar.copy(out=dst[:, split:, :], in_=src[:, split:, :])
 
         words = [pairs[u][:].rearrange("p t j -> p (t j)").bitcast(U32) for u in range(2)]
         picked = [keep.tile([P, 2, HALF], U32, name="picked%d" % h, tag="picked%d" % h, align_bytes=64) for h in range(2)]
-        woven = []
         x_codes = [keep.tile([P, HALF], U32, name="x_codes%d" % h, align_bytes=64) for h in range(2)]
         x_scales = [keep.tile([P, HALF], U8, name="x_scales%d" % h, align_bytes=64) for h in range(2)]
 
-        def gather_x(u, h):
-            nc.vector.tensor_copy(out=picked[h][:, u, :], in_=words[u].indirect(entries(h * HALF, (h + 1) * HALF)))
+        def gather_x(u, a, b):
+            h, o = divmod(a, HALF)
+            nc.vector.tensor_copy(out=picked[h][:, u, o : o + b - a], in_=words[u].indirect(entries(a, b)))
 
-        def weave(engine, h, a, b):
-            if not woven:
-                woven.append(keep.tile([P, S * PACK], BF16, name="woven", tag="w_raw0_0", align_bytes=64))
-            word = I32 if engine == "v" else U32
-            dst = woven[0][:].bitcast(word).rearrange("p (n u) -> p n u", u=2)[:, h * HALF + a : h * HALF + b, :]
-            src = picked[h][:].bitcast(word)[:, :, a:b].rearrange("p u n -> p n u")
-            if engine == "v":
-                nc.vector.tensor_copy(out=dst, in_=src)
-            else:
-                nc.scalar.copy(out=dst, in_=src)
+        lead = keep.tile([P, LEAD * PACK], BF16, name="lead", align_bytes=64)
 
-        def quantize_x(h):
-            nc.vector.quantize_mx(
-                out=x_codes[h][:].bitcast(FP8X4),
-                scales=x_scales[h][:],
-                in_=woven[0][:, h * HALF * PACK : (h + 1) * HALF * PACK],
+        def weave(copy, woven, a, b):
+            h, o = divmod(a, HALF)
+            copy(
+                out=woven.bitcast(U32).rearrange("p (n u) -> p n u", u=2),
+                in_=picked[h][:, :, o : o + b - a].rearrange("p u n -> p n u"),
             )
 
-        w_grouped = {}
+        def quantize_x(woven, a, b):
+            h, o = divmod(a, HALF)
+            nc.vector.quantize_mx(
+                out=x_codes[h][:, o : o + b - a].bitcast(FP8X4), scales=x_scales[h][:, o : o + b - a], in_=woven
+            )
+
         w_codes = [keep.tile([P, N], U32, name="w_codes%d" % i, align_bytes=64) for i in range(2)]
         w_scales = [keep.tile([P, N], U8, name="w_scales%d" % i, align_bytes=64) for i in range(2)]
 
         def group_w(i):
-            whole = keep.tile([P, N * PACK], BF16, name="w_grouped%d" % i, tag="w_grouped", align_bytes=64)
-            w_grouped[i] = whole[:]
-            for a, b in w_parts[i]:
+            grouped = keep.tile([P, N * PACK], BF16, name="w_grouped%d" % i, tag="w_grouped", align_bytes=64)
+            for a, b in W_PARTS[i]:
                 nc.scalar.copy(
-                    out=w_grouped[i][:, a * PACK : b * PACK].rearrange("p (c i t) -> p c t i", i=4, t=PACK),
-                    in_=w_raw[i, a][:].rearrange("p t (c i) -> p c t i", i=4),
+                    out=grouped[:][:, a * PACK : b * PACK].rearrange("p (c i j) -> p c j i", i=4, j=PACK),
+                    in_=w_raw[i, a][:].rearrange("p j (c i) -> p c j i", i=4),
                 )
+            return grouped
 
-        def quantize_w(i):
-            nc.vector.quantize_mx(
-                out=w_codes[i][:].bitcast(FP8X4),
-                scales=w_scales[i][:],
-                in_=w_grouped[i],
-            )
+        def quantize_w(i, grouped):
+            nc.vector.quantize_mx(out=w_codes[i][:].bitcast(FP8X4), scales=w_scales[i][:], in_=grouped[:])
 
-        vals = {}
+        def next_bank():
+            return psum.tile([P, HALF], F32, name="acc", tag="acc", bufs=ACC_BANKS)
 
-        def by_feature(i, mt, h, scale):
-            if (i, mt, h) == (0, 0, 1):
-                acc = psum.tile([P, HALF], F32, name="acc_low", tag="total")
-            else:
-                acc = psum.tile([P, HALF], F32, name="acc", tag="acc", bufs=4)
+        def by_feature(i, mt, h, scale, acc, value):
             nc.tensor.matmul_mx(
                 out=acc[:],
                 lhsT=w_codes[i][:, mt * P : (mt + 1) * P].bitcast(FP8X4),
@@ -130,150 +125,144 @@ def tile_picked_highway_tanh_l_kernel(tc, xT, res, w1, w2, offs, out):
                 start=True,
                 stop=True,
             )
-            if i == 0 and (mt, h) != (1, 1):
-                if (mt, h) == (0, 0):
-                    vals["first"] = keep.tile([P, 4 * HALF], F32, name="first", tag="w_raw1_0", align_bytes=64)
-                slot = mt + 2 * h
-                v = vals["first"][:, slot * HALF : (slot + 1) * HALF]
-            else:
-                whole = keep.tile([P, HALF], F32, name="val%d%d%d" % (i, mt, h))
-                v = whole[:]
-            nc.scalar.activation(v, acc[:], ACT.Tanh, scale=scale)
-            vals[i, mt, h] = v
+            nc.scalar.activation(value, acc[:], ACT.Tanh, scale=scale)
 
-        def by_token(h):
-            acc = psum.tile([P, HALF], F32, name="acc", tag="acc", bufs=4)
-            for t in range(BLOCKS):
-                cols = slice(t * P, (t + 1) * P)
+        def gate_by_entry(acc, value):
+            for block in range(HALF // P):
+                cols = slice(block * P, (block + 1) * P)
                 nc.tensor.matmul_mx(
                     out=acc[:, cols],
-                    lhsT=x_codes[h][:, cols].bitcast(FP8X4),
-                    lhsT_scale=x_scales[h][:, cols],
-                    rhs=w_codes[1][:, 0:P].bitcast(FP8X4),
-                    rhs_scale=w_scales[1][:, 0:P],
+                    lhsT=x_codes[1][:, cols].bitcast(FP8X4),
+                    lhsT_scale=x_scales[1][:, cols],
+                    rhs=w_codes[GATE][:, 0:P].bitcast(FP8X4),
+                    rhs_scale=w_scales[GATE][:, 0:P],
                     start=True,
                     stop=True,
                 )
-            v = keep.tile([P, HALF], F32, name="gate_t%d" % h)
-            nc.scalar.activation(v[:], acc[:], ACT.Tanh, scale=0.5)
-            vals[1, 0, h] = v
+            nc.scalar.activation(value, acc[:], ACT.Tanh, scale=0.5)
 
-        def turn(bank, src, first, last):
-            for t in range(BLOCKS):
-                cols = slice(t * P, (t + 1) * P)
+        def turn(bank, src, width, first, last):
+            blocks = width // P
+            for block in range(blocks):
+                cols = slice(block * P, (block + 1) * P)
                 nc.tensor.matmul(
                     bank[:, cols], src[:, cols], ident[:], is_transpose=True,
-                    start=(first and t == 0), stop=(last and t == BLOCKS - 1),
+                    start=(first and block == 0), stop=(last and block == blocks - 1),
                 )
 
-        diff, total, pull = {}, {}, {}
+        def fresh(name, width):
+            tile = keep.tile([P, width], F32, name=name)
+            return tile[:]
 
-        passed = {}
+        def gather_difference(d, mt, a, b, y, op):
+            nc.vector.tensor_tensor(d, res_rows[mt][:].indirect(entries(a, b)), y, op)
 
-        def look_up(h):
-            whole = keep.tile([P, HALF], F32, name="passed%d" % h, tag="picked0", align_bytes=64)
-            passed[h] = whole[:]
-            nc.vector.tensor_copy(out=passed[h], in_=res_rows[0][:].indirect(entries(h * HALF, (h + 1) * HALF)))
+        def weigh(e, t, one, d):
+            nc.vector.scalar_tensor_tensor(out=e, in0=t, scalar=one, in1=d, op0=ALU.add, op1=ALU.mult)
 
-        passed_t = {}
+        def finish(mt, a, b, e, y, op):
+            result = fresh("result%d_%d" % (mt, a), b - a)
+            nc.vector.scalar_tensor_tensor(out=result, in0=e, scalar=-0.5, in1=y, op0=ALU.mult, op1=op)
+            nc.sync.dma_start(out=out[mt * P : (mt + 1) * P, a:b], in_=result)
 
-        def turn_passed(h):
-            turned = psum.tile([P, HALF], F32, name="turned", tag="diff")
-            turn(turned, passed[h], True, True)
-            rt = vals["first"][:, 3 * HALF : 4 * HALF]
-            nc.scalar.activation(rt, turned[:], ACT.Copy, scale=-2.0)
-            passed_t[h] = rt
+        low = keep.tile([P, S - PIECE], F32, name="low")
 
-        def difference(h):
-            diff[h] = psum.tile([P, HALF], F32, name="diff", tag="diff")
-            turn(diff[h], passed[h], True, False)
-            turn(diff[h], vals[0, 0, h], False, True)
+        round_load(0)
+        round_load(1)
+        gather_x(0, 0, HALF)
+        gather_x(0, HALF, S)
+        round_load(2)
+        round_load(3)
+        round_load(4)
+        for a in range(0, S, PIECE):
+            gather_x(1, a, a + PIECE)
 
-        def weigh(h):
-            e = keep.tile([P, HALF], F32, name="pull%d" % h)
-            nc.vector.scalar_tensor_tensor(out=e[:], in0=vals[1, 0, h][:], scalar=1.0, in1=diff[h][:], op0=ALU.add, op1=ALU.mult)
-            total[h] = psum.tile([P, HALF], F32, name="total", tag="total")
-            turn(total[h], passed_t[h], True, False)
-            turn(total[h], e, False, True)
+        w1_grouped = group_w(LAYER)
+        weave(nc.gpsimd.tensor_copy, lead[:], 0, LEAD)
+        woven = keep.tile([P, (S - LEAD) * PACK], BF16, name="woven", tag="w_raw0_0", align_bytes=64)
+        woven_first = woven[:, 0 : (HALF - LEAD) * PACK]
+        woven_second = woven[:, (HALF - LEAD) * PACK :]
+        weave(nc.scalar.copy, woven_first, LEAD, HALF)
+        weave(nc.scalar.copy, woven_second[:, 0 : PIECE * PACK], HALF, HALF + PIECE)
+        weave(nc.scalar.copy, woven_second[:, PIECE * PACK :], HALF + PIECE, S)
+        quantize_x(lead[:], 0, LEAD)
+        quantize_w(LAYER, w1_grouped)
+        quantize_x(woven_first, LEAD, HALF)
+        w2_grouped = group_w(GATE)
 
-        def finish_low(h):
-            y = keep.tile([P, HALF], F32, name="low%d" % h)
-            nc.scalar.activation(y[:], total[h][:], ACT.Copy, scale=-0.5)
-            nc.sync.dma_start(out=out[0:P, h * HALF : (h + 1) * HALF], in_=y[:])
+        r01_tile = keep.tile([P, HALF], F32, name="r01", tag="picked0", align_bytes=64)
+        r01 = r01_tile[:]
+        nc.vector.tensor_copy(out=r01, in_=res_rows[0][:].indirect(entries(HALF, S)))
 
-        gap, part = {}, {}
+        bank = next_bank()
+        early = keep.tile([P, 4 * HALF], F32, name="early", tag="w_raw1_0", align_bytes=64)
+        neg_y00, y10, neg_y01, r01_turned = [early[:, n * HALF : (n + 1) * HALF] for n in range(4)]
+        by_feature(LAYER, 0, 0, -1.0, bank, neg_y00)
+        by_feature(LAYER, 1, 0, 1.0, next_bank(), y10)
+        quantize_x(woven_second, HALF, S)
+        quantize_w(GATE, w2_grouped)
 
-        def carry(mt, a, b):
-            h, o = divmod(a, HALF)
-            if (mt, a) == (1, 768):
-                q = vals[1, 1, 0][:, 0 : b - a]
-            else:
-                q = keep.tile([P, b - a], F32, name="gap%d_%d" % (mt, a))
-            nc.vector.tensor_tensor(
-                q[:], res_rows[mt][:].indirect(entries(a, b)), vals[0, mt, h][:, o : o + b - a], ALU.subtract
-            )
-            gap[mt, a] = q
+        turned = psum.tile([P, HALF], F32, name="turned", tag="diff")
+        turn(turned, r01, HALF, True, True)
+        nc.scalar.activation(r01_turned, turned[:], ACT.Copy, scale=-2.0)
+        by_feature(LAYER, 0, 1, -1.0, psum.tile([P, HALF], F32, name="acc_low", tag="total"), neg_y01)
 
-        def gate(mt, a, b):
-            h, o = divmod(a, HALF)
-            cols = slice(o, o + b - a)
-            g = keep.tile([P, b - a], F32, name="part%d_%d" % (mt, a))
-            nc.vector.scalar_tensor_tensor(
-                out=g[:], in0=vals[1, mt, h][:, cols], scalar=-1.0, in1=gap[mt, a][:], op0=ALU.add, op1=ALU.mult
-            )
-            part[mt, a] = g
+        d00 = fresh("d00", HALF)
+        gather_difference(d00, 0, 0, HALF, neg_y00, ALU.add)
+        bank = next_bank()
+        t00 = fresh("t00", HALF)
+        by_feature(GATE, 0, 0, 0.5, bank, t00)
+        bank = next_bank()
+        t01 = fresh("t01", HALF)
+        gate_by_entry(bank, t01)
+        d01 = psum.tile([P, HALF], F32, name="d01", tag="diff")
+        turn(d01, r01, HALF, True, False)
+        turn(d01, neg_y01, HALF, False, True)
+        total = psum.tile([P, HALF], F32, name="total", tag="total")
+        turn(total, r01_turned, HALF, True, False)
 
-        def finish(mt, a, b, first):
-            h, o = divmod(a, HALF)
-            y = keep.tile([P, b - a], F32, name="result%d_%d" % (mt, a))
-            nc.vector.scalar_tensor_tensor(
-                out=y[:], in0=part[mt, first][:, a - first : b - first], scalar=-0.5, in1=vals[0, mt, h][:, o : o + b - a], op0=ALU.mult, op1=ALU.add
-            )
-            nc.sync.dma_start(out=out[mt * P : (mt + 1) * P, a:b], in_=y[:])
+        d10 = fresh("d10", HALF)
+        gather_difference(d10, 1, 0, HALF, y10, ALU.subtract)
+        bank = next_bank()
+        t10 = fresh("t10", HALF)
+        by_feature(GATE, 1, 0, 0.5, bank, t10)
+        bank = next_bank()
+        y11 = fresh("y11", HALF)
+        by_feature(LAYER, 1, 1, 1.0, bank, y11)
 
-        cast("s", 0, 0, 1024)
-        cast("v", 1, 0, 704)
-        cast("s", 1, 704, 1024)
-        gather_x(0, 0)
-        gather_x(0, 1)
-        cast("s", 2, 0, 768)
-        cast("v", 3, 0, 576)
-        cast("s", 3, 576, 896)
-        cast("v", 4, 0, 256)
-        cast("s", 4, 256, 384)
-        gather_x(1, 0)
-        gather_x(1, 1)
-        group_w(0)
-        weave("s", 0, 0, 384)
-        weave("v", 0, 384, 512)
-        weave("s", 1, 0, 512)
-        quantize_w(0)
-        quantize_x(0)
-        group_w(1)
-        look_up(1)
-        by_feature(0, 0, 0, 1.0)
-        by_feature(0, 1, 0, 1.0)
-        quantize_x(1)
-        quantize_w(1)
-        turn_passed(1)
-        by_feature(0, 0, 1, -1.0)
-        carry(0, 0, 512)
-        by_feature(1, 0, 0, 0.5)
-        by_token(1)
-        difference(1)
-        carry(1, 0, 512)
-        by_feature(1, 1, 0, 0.5)
-        by_feature(0, 1, 1, 1.0)
-        gate(0, 0, 512)
-        weigh(1)
-        by_feature(1, 1, 1, 0.5)
-        finish(0, 0, 512, 0)
-        finish_low(1)
-        gate(1, 0, 512)
-        carry(1, 512, 768)
-        finish(1, 0, 512, 0)
-        carry(1, 768, 1024)
-        gate(1, 512, 768)
-        gate(1, 768, 1024)
-        finish(1, 512, 768, 512)
-        finish(1, 768, 1024, 768)
+        e00 = fresh("e00", HALF)
+        weigh(e00, t00, -1.0, d00)
+        summed = psum.tile([P, HALF], F32, name="summed")
+        turn(summed, neg_y00[:, PIECE:], PIECE, True, False)
+        turn(summed, neg_y00[:, PIECE:], PIECE, False, False)
+        turn(summed, e00[:, PIECE:], PIECE, False, True)
+        out00_turned = fresh("out00_turned", PIECE)
+        nc.scalar.activation(out00_turned, summed[:, 0:PIECE], ACT.Copy, scale=-0.5)
+
+        e01 = fresh("e01", HALF)
+        weigh(e01, t01, 1.0, d01[:])
+        turn(total, e01, HALF, False, True)
+        bank = next_bank()
+        t11 = fresh("t11", HALF)
+        by_feature(GATE, 1, 1, 0.5, bank, t11)
+
+        finish(0, 0, PIECE, e00[:, 0:PIECE], neg_y00[:, 0:PIECE], ALU.subtract)
+        nc.scalar.activation(low[:, PIECE:], total[:], ACT.Copy, scale=-0.5)
+        back = psum.tile([P, HALF], F32, name="back", tag="diff")
+        turn(back, out00_turned, PIECE, True, True)
+        nc.scalar.copy(out=low[:, 0:PIECE], in_=back[:, 0:PIECE])
+        nc.sync.dma_start(out=out[0:P, PIECE:S], in_=low[:])
+
+        e10 = fresh("e10", HALF)
+        weigh(e10, t10, -1.0, d10)
+        d11_a = fresh("d11_a", PIECE)
+        gather_difference(d11_a, 1, HALF, HALF + PIECE, y11[:, 0:PIECE], ALU.subtract)
+        finish(1, 0, HALF, e10, y10, ALU.add)
+        d11_b = t10[:, 0:PIECE]
+        gather_difference(d11_b, 1, HALF + PIECE, S, y11[:, PIECE:], ALU.subtract)
+        e11_a = fresh("e11_a", PIECE)
+        weigh(e11_a, t11[:, 0:PIECE], -1.0, d11_a)
+        e11_b = fresh("e11_b", PIECE)
+        weigh(e11_b, t11[:, PIECE:], -1.0, d11_b)
+        finish(1, HALF, HALF + PIECE, e11_a, y11[:, 0:PIECE], ALU.add)
+        finish(1, HALF + PIECE, S, e11_b, y11[:, PIECE:], ALU.add)

@@ -23,11 +23,6 @@ PIECE = 256
 ACC_BANKS = 4
 LAYER, GATE = 0, 1
 
-X_LOADS = [(0, 0, 1024), (0, 1024, 2048), (1, 0, 768), (1, 768, 1664), (1, 1664, 2048)]
-VECTOR_COLUMNS = [0, 704, 0, 576, 256]
-W_PARTS = [[(0, N)], [(0, P), (P, N)]]
-LEAD = PIECE
-
 
 def tile_picked_highway_tanh_l_kernel(tc, xT, res, w1, w2, offs, out):
     nc = tc.nc
@@ -42,71 +37,67 @@ def tile_picked_highway_tanh_l_kernel(tc, xT, res, w1, w2, offs, out):
         def entries(a, b):
             return offsets[:, a // LIST_ROWS : b // LIST_ROWS]
 
+        def fresh(name, width, tag=None):
+            tile = keep.tile([P, width], F32, name=name, tag=tag or name)
+            return tile[:]
+
         ident = keep.tile([P, P], F32, name="ident")
         make_identity(nc, ident[:])
 
-        res_rows = [keep.tile([P, T], F32, name="res%d" % mt) for mt in range(2)]
-        x_raw = []
-        for i, (u, a, b) in enumerate(X_LOADS):
-            raw = keep.tile([P, 2, b - a], F32, name="x_raw%d" % i)
-            nc.sync.dma_start(out=raw[:], in_=x_rows[:, 2 * u : 2 * u + 2, a:b])
-            x_raw.append(raw)
-            if i == 0:
+        zero = keep.tile([P, 1], F32, name="zero")
+        nc.gpsimd.memset(zero[:], 0.0)
+        half = keep.tile([P, 1], F32, name="half")
+        nc.scalar.activation(half[:], zero[:], ACT.Sigmoid)
+
+        planes = []
+        for j in range(PACK):
+            plane = keep.tile([P, T], F32, name="plane%d" % j)
+            nc.sync.dma_start(out=plane[:], in_=x_rows[:, j, :])
+            planes.append(plane)
+            if j == 0:
                 nc.sync.dma_start(offsets[:], offs)
-        w_raw = {}
+        w_raw = []
         for i, w in enumerate((w1, w2)):
-            for a, b in W_PARTS[i]:
-                w_raw[i, a] = keep.tile(
-                    [P, PACK, b - a], F32, name="w_raw%d_%d" % (i, a), tag="w_raw%d_%d" % (i, a), align_bytes=64
-                )
-                nc.sync.dma_start(out=w_raw[i, a][:], in_=w.rearrange("(p j) n -> p j n", j=PACK)[:, :, a:b])
-            nc.sync.dma_start(out=res_rows[i][:], in_=res[i * P : (i + 1) * P, :])
+            raw = keep.tile([P, PACK, N], F32, name="w_raw%d" % i, align_bytes=64)
+            nc.sync.dma_start(out=raw[:], in_=w.rearrange("(p j) n -> p j n", j=PACK))
+            w_raw.append(raw)
+        res_rows = [keep.tile([P, T], F32, name="res%d" % mt) for mt in range(2)]
+        for mt in range(2):
+            nc.sync.dma_start(out=res_rows[mt][:], in_=res[mt * P : (mt + 1) * P, :])
 
-        pairs = [keep.tile([P, T, 2], BF16, name="pairs%d" % u) for u in range(2)]
-
-        def round_load(i):
-            u, a, b = X_LOADS[i]
-            src = x_raw[i][:].rearrange("p j c -> p c j")
-            dst = pairs[u][:, a:b, :]
-            split = VECTOR_COLUMNS[i]
-            if split:
-                nc.vector.tensor_copy(out=dst[:, 0:split, :], in_=src[:, 0:split, :])
-            nc.scalar.copy(out=dst[:, split:, :], in_=src[:, split:, :])
-
-        words = [pairs[u][:].rearrange("p t j -> p (t j)").bitcast(U32) for u in range(2)]
-        picked = [keep.tile([P, 2, HALF], U32, name="picked%d" % h, tag="picked%d" % h, align_bytes=64) for h in range(2)]
-        x_codes = [keep.tile([P, HALF], U32, name="x_codes%d" % h, align_bytes=64) for h in range(2)]
+        direct = [keep.tile([P, PIECE, PACK], BF16, name="direct%d" % n, align_bytes=64) for n in range(2)]
+        woven = keep.tile([P, HALF, PACK], BF16, name="woven", align_bytes=64)
+        flat = [keep.tile([P, 2, HALF], BF16, name="flat%d" % u, align_bytes=64) for u in range(2)]
+        x_codes = {0: keep.tile([P, HALF], U32, name="x_codes0", align_bytes=64)}
         x_scales = [keep.tile([P, HALF], U8, name="x_scales%d" % h, align_bytes=64) for h in range(2)]
 
-        def gather_x(u, a, b):
-            h, o = divmod(a, HALF)
-            nc.vector.tensor_copy(out=picked[h][:, u, o : o + b - a], in_=words[u].indirect(entries(a, b)))
+        def gather_plane(j):
+            for n in range(2):
+                nc.vector.tensor_copy(
+                    out=direct[n][:, :, j], in_=planes[j][:].indirect(entries(n * PIECE, (n + 1) * PIECE))
+                )
+            nc.scalar.activation(flat[j // 2][:, j % 2, :], planes[j][:].indirect(entries(HALF, S)), ACT.Copy)
 
-        lead = keep.tile([P, LEAD * PACK], BF16, name="lead", align_bytes=64)
+        def insert(u):
+            nc.vector.tensor_copy(out=woven[:, :, 2 * u : 2 * u + 2], in_=flat[u][:].rearrange("p j n -> p n j"))
 
-        def weave(copy, woven, a, b):
-            h, o = divmod(a, HALF)
-            copy(
-                out=woven.bitcast(U32).rearrange("p (n u) -> p n u", u=2),
-                in_=picked[h][:, :, o : o + b - a].rearrange("p u n -> p n u"),
-            )
-
-        def quantize_x(woven, a, b):
+        def quantize_x(src, a, b):
             h, o = divmod(a, HALF)
             nc.vector.quantize_mx(
-                out=x_codes[h][:, o : o + b - a].bitcast(FP8X4), scales=x_scales[h][:, o : o + b - a], in_=woven
+                out=x_codes[h][:, o : o + b - a].bitcast(FP8X4),
+                scales=x_scales[h][:, o : o + b - a],
+                in_=src[:].rearrange("p n j -> p (n j)"),
             )
 
         w_codes = [keep.tile([P, N], U32, name="w_codes%d" % i, align_bytes=64) for i in range(2)]
         w_scales = [keep.tile([P, N], U8, name="w_scales%d" % i, align_bytes=64) for i in range(2)]
 
         def group_w(i):
-            grouped = keep.tile([P, N * PACK], BF16, name="w_grouped%d" % i, tag="w_grouped", align_bytes=64)
-            for a, b in W_PARTS[i]:
-                nc.scalar.copy(
-                    out=grouped[:][:, a * PACK : b * PACK].rearrange("p (c i j) -> p c j i", i=4, j=PACK),
-                    in_=w_raw[i, a][:].rearrange("p j (c i) -> p c j i", i=4),
-                )
+            grouped = keep.tile([P, N * PACK], BF16, name="w_grouped%d" % i, tag="w_grouped%d" % i, align_bytes=64)
+            nc.scalar.copy(
+                out=grouped[:].rearrange("p (c i j) -> p c j i", i=4, j=PACK),
+                in_=w_raw[i][:].rearrange("p j (c i) -> p c j i", i=4),
+            )
             return grouped
 
         def quantize_w(i, grouped):
@@ -115,7 +106,9 @@ def tile_picked_highway_tanh_l_kernel(tc, xT, res, w1, w2, offs, out):
         def next_bank():
             return psum.tile([P, HALF], F32, name="acc", tag="acc", bufs=ACC_BANKS)
 
-        def by_feature(i, mt, h, scale, acc, value):
+        def by_feature(i, mt, h, scale, name):
+            acc = next_bank()
+            value = fresh(name, HALF)
             nc.tensor.matmul_mx(
                 out=acc[:],
                 lhsT=w_codes[i][:, mt * P : (mt + 1) * P].bitcast(FP8X4),
@@ -126,20 +119,24 @@ def tile_picked_highway_tanh_l_kernel(tc, xT, res, w1, w2, offs, out):
                 stop=True,
             )
             nc.scalar.activation(value, acc[:], ACT.Tanh, scale=scale)
+            return value
 
-        def gate_by_entry(acc, value):
+        def gate_by_entry(mt, h, func, scale, name):
+            acc = next_bank()
+            value = fresh(name, HALF)
             for block in range(HALF // P):
                 cols = slice(block * P, (block + 1) * P)
                 nc.tensor.matmul_mx(
                     out=acc[:, cols],
-                    lhsT=x_codes[1][:, cols].bitcast(FP8X4),
-                    lhsT_scale=x_scales[1][:, cols],
-                    rhs=w_codes[GATE][:, 0:P].bitcast(FP8X4),
-                    rhs_scale=w_scales[GATE][:, 0:P],
+                    lhsT=x_codes[h][:, cols].bitcast(FP8X4),
+                    lhsT_scale=x_scales[h][:, cols],
+                    rhs=w_codes[GATE][:, mt * P : (mt + 1) * P].bitcast(FP8X4),
+                    rhs_scale=w_scales[GATE][:, mt * P : (mt + 1) * P],
                     start=True,
                     stop=True,
                 )
-            nc.scalar.activation(value, acc[:], ACT.Tanh, scale=0.5)
+            nc.scalar.activation(value, acc[:], func, scale=scale)
+            return value
 
         def turn(bank, src, width, first, last):
             blocks = width // P
@@ -150,119 +147,83 @@ def tile_picked_highway_tanh_l_kernel(tc, xT, res, w1, w2, offs, out):
                     start=(first and block == 0), stop=(last and block == blocks - 1),
                 )
 
-        def fresh(name, width):
-            tile = keep.tile([P, width], F32, name=name)
-            return tile[:]
+        def weigh(name, t, d, width):
+            e = fresh(name, width)
+            nc.vector.scalar_tensor_tensor(out=e, in0=t, scalar=-1.0, in1=d, op0=ALU.add, op1=ALU.mult)
+            return e
 
-        def gather_difference(d, mt, a, b, y, op):
-            nc.vector.tensor_tensor(d, res_rows[mt][:].indirect(entries(a, b)), y, op)
-
-        def weigh(e, t, one, d):
-            nc.vector.scalar_tensor_tensor(out=e, in0=t, scalar=one, in1=d, op0=ALU.add, op1=ALU.mult)
-
-        def finish(mt, a, b, e, y, op):
+        def finish(mt, a, b, e, neg_y):
             result = fresh("result%d_%d" % (mt, a), b - a)
-            nc.vector.scalar_tensor_tensor(out=result, in0=e, scalar=-0.5, in1=y, op0=ALU.mult, op1=op)
+            nc.vector.scalar_tensor_tensor(out=result, in0=e, scalar=-0.5, in1=neg_y, op0=ALU.mult, op1=ALU.subtract)
             nc.sync.dma_start(out=out[mt * P : (mt + 1) * P, a:b], in_=result)
 
-        low = keep.tile([P, S - PIECE], F32, name="low")
-
-        round_load(0)
-        round_load(1)
-        gather_x(0, 0, HALF)
-        gather_x(0, HALF, S)
-        round_load(2)
-        round_load(3)
-        round_load(4)
-        for a in range(0, S, PIECE):
-            gather_x(1, a, a + PIECE)
-
+        gather_plane(0)
+        gather_plane(1)
+        insert(0)
+        gather_plane(2)
+        gather_plane(3)
         w1_grouped = group_w(LAYER)
-        weave(nc.gpsimd.tensor_copy, lead[:], 0, LEAD)
-        woven = keep.tile([P, (S - LEAD) * PACK], BF16, name="woven", tag="w_raw0_0", align_bytes=64)
-        woven_first = woven[:, 0 : (HALF - LEAD) * PACK]
-        woven_second = woven[:, (HALF - LEAD) * PACK :]
-        weave(nc.scalar.copy, woven_first, LEAD, HALF)
-        weave(nc.scalar.copy, woven_second[:, 0 : PIECE * PACK], HALF, HALF + PIECE)
-        weave(nc.scalar.copy, woven_second[:, PIECE * PACK :], HALF + PIECE, S)
-        quantize_x(lead[:], 0, LEAD)
-        quantize_w(LAYER, w1_grouped)
-        quantize_x(woven_first, LEAD, HALF)
         w2_grouped = group_w(GATE)
-
-        r01_tile = keep.tile([P, HALF], F32, name="r01", tag="picked0", align_bytes=64)
-        r01 = r01_tile[:]
-        nc.vector.tensor_copy(out=r01, in_=res_rows[0][:].indirect(entries(HALF, S)))
-
-        bank = next_bank()
-        early = keep.tile([P, 4 * HALF], F32, name="early", tag="w_raw1_0", align_bytes=64)
-        neg_y00, y10, neg_y01, r01_turned = [early[:, n * HALF : (n + 1) * HALF] for n in range(4)]
-        by_feature(LAYER, 0, 0, -1.0, bank, neg_y00)
-        by_feature(LAYER, 1, 0, 1.0, next_bank(), y10)
-        quantize_x(woven_second, HALF, S)
+        quantize_x(direct[0], 0, PIECE)
+        quantize_x(direct[1], PIECE, HALF)
+        quantize_w(LAYER, w1_grouped)
+        insert(1)
+        x_codes[1] = keep.tile([P, HALF], U32, name="x_codes1", tag="w_grouped0", align_bytes=64)
+        quantize_x(woven, HALF, S)
         quantize_w(GATE, w2_grouped)
 
-        turned = psum.tile([P, HALF], F32, name="turned", tag="diff")
-        turn(turned, r01, HALF, True, True)
-        nc.scalar.activation(r01_turned, turned[:], ACT.Copy, scale=-2.0)
-        by_feature(LAYER, 0, 1, -1.0, psum.tile([P, HALF], F32, name="acc_low", tag="total"), neg_y01)
+        neg_y = {}
+        gate = {}
+        neg_y[0, 0] = by_feature(LAYER, 0, 0, -1.0, "y00")
+        neg_y[0, 1] = by_feature(LAYER, 0, 1, -1.0, "y01")
+        gate[0, 0] = gate_by_entry(0, 0, ACT.Sigmoid, -1.0, "s00")
+        gate[0, 1] = gate_by_entry(0, 1, ACT.Sigmoid, -1.0, "s01")
+        neg_y[1, 1] = by_feature(LAYER, 1, 1, -1.0, "y11")
+        gate[1, 1] = gate_by_entry(1, 1, ACT.Tanh, half[:], "t11")
+        neg_y[1, 0] = by_feature(LAYER, 1, 0, -1.0, "y10")
+        gate[1, 0] = gate_by_entry(1, 0, ACT.Tanh, half[:], "t10")
 
-        d00 = fresh("d00", HALF)
-        gather_difference(d00, 0, 0, HALF, neg_y00, ALU.add)
-        bank = next_bank()
-        t00 = fresh("t00", HALF)
-        by_feature(GATE, 0, 0, 0.5, bank, t00)
-        bank = next_bank()
-        t01 = fresh("t01", HALF)
-        gate_by_entry(bank, t01)
-        d01 = psum.tile([P, HALF], F32, name="d01", tag="diff")
-        turn(d01, r01, HALF, True, False)
-        turn(d01, neg_y01, HALF, False, True)
-        total = psum.tile([P, HALF], F32, name="total", tag="total")
-        turn(total, r01_turned, HALF, True, False)
+        d = {}
+        s_back = {}
+        for h in range(2):
+            d[h] = fresh("d0%d" % h, HALF)
+            nc.vector.tensor_tensor(d[h], res_rows[0][:].indirect(entries(h * HALF, (h + 1) * HALF)), neg_y[0, h], ALU.add)
+            s_back[h] = psum.tile([P, HALF], F32, name="s_back%d" % h, tag="side%d" % h)
+            turn(s_back[h], gate[0, h], HALF, True, True)
+        for h in range(2):
+            e = fresh("e0%d" % h, HALF)
+            nc.vector.tensor_tensor(e, s_back[h][:], d[h], ALU.mult)
+            result = fresh("result0%d" % h, HALF)
+            nc.gpsimd.tensor_tensor(result, e, neg_y[0, h], ALU.subtract)
+            nc.sync.dma_start(out=out[0:P, h * HALF : (h + 1) * HALF], in_=result)
 
-        d10 = fresh("d10", HALF)
-        gather_difference(d10, 1, 0, HALF, y10, ALU.subtract)
-        bank = next_bank()
-        t10 = fresh("t10", HALF)
-        by_feature(GATE, 1, 0, 0.5, bank, t10)
-        bank = next_bank()
-        y11 = fresh("y11", HALF)
-        by_feature(LAYER, 1, 1, 1.0, bank, y11)
+        def part(tiles, n):
+            h, o = divmod(n * PIECE, HALF)
+            return tiles[1, h][:, o : o + PIECE]
 
-        e00 = fresh("e00", HALF)
-        weigh(e00, t00, -1.0, d00)
-        summed = psum.tile([P, HALF], F32, name="summed")
-        turn(summed, neg_y00[:, PIECE:], PIECE, True, False)
-        turn(summed, neg_y00[:, PIECE:], PIECE, False, False)
-        turn(summed, e00[:, PIECE:], PIECE, False, True)
-        out00_turned = fresh("out00_turned", PIECE)
-        nc.scalar.activation(out00_turned, summed[:, 0:PIECE], ACT.Copy, scale=-0.5)
-
-        e01 = fresh("e01", HALF)
-        weigh(e01, t01, 1.0, d01[:])
-        turn(total, e01, HALF, False, True)
-        bank = next_bank()
-        t11 = fresh("t11", HALF)
-        by_feature(GATE, 1, 1, 0.5, bank, t11)
-
-        finish(0, 0, PIECE, e00[:, 0:PIECE], neg_y00[:, 0:PIECE], ALU.subtract)
-        nc.scalar.activation(low[:, PIECE:], total[:], ACT.Copy, scale=-0.5)
-        back = psum.tile([P, HALF], F32, name="back", tag="diff")
-        turn(back, out00_turned, PIECE, True, True)
-        nc.scalar.copy(out=low[:, 0:PIECE], in_=back[:, 0:PIECE])
-        nc.sync.dma_start(out=out[0:P, PIECE:S], in_=low[:])
-
-        e10 = fresh("e10", HALF)
-        weigh(e10, t10, -1.0, d10)
-        d11_a = fresh("d11_a", PIECE)
-        gather_difference(d11_a, 1, HALF, HALF + PIECE, y11[:, 0:PIECE], ALU.subtract)
-        finish(1, 0, HALF, e10, y10, ALU.add)
-        d11_b = t10[:, 0:PIECE]
-        gather_difference(d11_b, 1, HALF + PIECE, S, y11[:, PIECE:], ALU.subtract)
-        e11_a = fresh("e11_a", PIECE)
-        weigh(e11_a, t11[:, 0:PIECE], -1.0, d11_a)
-        e11_b = fresh("e11_b", PIECE)
-        weigh(e11_b, t11[:, PIECE:], -1.0, d11_b)
-        finish(1, HALF, HALF + PIECE, e11_a, y11[:, 0:PIECE], ALU.add)
-        finish(1, HALF + PIECE, S, e11_b, y11[:, PIECE:], ALU.add)
+        order = [2, 0, 3, 1]
+        diff = {}
+        back = {}
+        for n in order:
+            if n >= 2:
+                diff[n] = psum.tile([P, HALF], F32, name="diff%d" % n)
+            else:
+                diff[n] = next_bank()
+            turn(diff[n], part(neg_y, n), PIECE, True, False)
+        for n in order:
+            r = fresh("r1_%d" % n, PIECE)
+            window = res_rows[1][:].indirect(entries(n * PIECE, (n + 1) * PIECE))
+            if n >= 2:
+                nc.vector.tensor_copy(out=r, in_=window)
+            else:
+                nc.scalar.activation(r, window, ACT.Copy)
+            turn(diff[n], r, PIECE, False, True)
+        for place, n in enumerate(order):
+            e_turned = weigh("e1_%d" % n, part(gate, n), diff[n][:, 0:PIECE], PIECE)
+            if place < 2:
+                back[n] = psum.tile([P, HALF], F32, name="back%d" % n, tag="side%d" % place)
+            else:
+                back[n] = next_bank()
+            turn(back[n], e_turned, PIECE, True, True)
+        for n in order:
+            finish(1, n * PIECE, (n + 1) * PIECE, back[n][:, 0:PIECE], part(neg_y, n))

@@ -22,6 +22,7 @@ HALF = 512
 PIECE = 256
 ACC_BANKS = 4
 LAYER, GATE = 0, 1
+DIRECT = 384
 
 
 def tile_picked_highway_tanh_l_kernel(tc, xT, res, w1, w2, offs, out):
@@ -65,21 +66,23 @@ def tile_picked_highway_tanh_l_kernel(tc, xT, res, w1, w2, offs, out):
         for mt in range(2):
             nc.sync.dma_start(out=res_rows[mt][:], in_=res[mt * P : (mt + 1) * P, :])
 
-        direct = [keep.tile([P, PIECE, PACK], BF16, name="direct%d" % n, align_bytes=64) for n in range(2)]
-        woven = keep.tile([P, HALF, PACK], BF16, name="woven", align_bytes=64)
-        flat = [keep.tile([P, 2, HALF], BF16, name="flat%d" % u, align_bytes=64) for u in range(2)]
+        direct = keep.tile([P, DIRECT, PACK], BF16, name="direct", align_bytes=64)
+        spans = [(DIRECT, HALF), (HALF, S)]
+        woven = [keep.tile([P, b - a, PACK], BF16, name="woven%d" % a, align_bytes=64) for a, b in spans]
+        flat = [
+            [keep.tile([P, 2, b - a], BF16, name="flat%d_%d" % (u, a), align_bytes=64) for a, b in spans]
+            for u in range(2)
+        ]
         x_codes = {0: keep.tile([P, HALF], U32, name="x_codes0", align_bytes=64)}
         x_scales = [keep.tile([P, HALF], U8, name="x_scales%d" % h, align_bytes=64) for h in range(2)]
 
         def gather_plane(j):
-            for n in range(2):
-                nc.vector.tensor_copy(
-                    out=direct[n][:, :, j], in_=planes[j][:].indirect(entries(n * PIECE, (n + 1) * PIECE))
-                )
-            nc.scalar.activation(flat[j // 2][:, j % 2, :], planes[j][:].indirect(entries(HALF, S)), ACT.Copy)
+            nc.vector.tensor_copy(out=direct[:, :, j], in_=planes[j][:].indirect(entries(0, DIRECT)))
+            for n, (a, b) in enumerate(spans):
+                nc.scalar.activation(flat[j // 2][n][:, j % 2, :], planes[j][:].indirect(entries(a, b)), ACT.Copy)
 
-        def insert(u):
-            nc.vector.tensor_copy(out=woven[:, :, 2 * u : 2 * u + 2], in_=flat[u][:].rearrange("p j n -> p n j"))
+        def insert(u, n):
+            nc.vector.tensor_copy(out=woven[n][:, :, 2 * u : 2 * u + 2], in_=flat[u][n][:].rearrange("p j n -> p n j"))
 
         def quantize_x(src, a, b):
             h, o = divmod(a, HALF)
@@ -91,22 +94,24 @@ def tile_picked_highway_tanh_l_kernel(tc, xT, res, w1, w2, offs, out):
 
         w_codes = [keep.tile([P, N], U32, name="w_codes%d" % i, align_bytes=64) for i in range(2)]
         w_scales = [keep.tile([P, N], U8, name="w_scales%d" % i, align_bytes=64) for i in range(2)]
+        w_grouped = {}
 
-        def group_w(i):
-            grouped = keep.tile([P, N * PACK], BF16, name="w_grouped%d" % i, tag="w_grouped%d" % i, align_bytes=64)
-            nc.scalar.copy(
-                out=grouped[:].rearrange("p (c i j) -> p c j i", i=4, j=PACK),
-                in_=w_raw[i][:].rearrange("p j (c i) -> p c j i", i=4),
+        def group_w(copy, i, mt):
+            name = "w_grouped%d%d" % (i, mt)
+            w_grouped[i, mt] = keep.tile([P, P * PACK], BF16, name=name, tag=name, align_bytes=64)
+            copy(
+                out=w_grouped[i, mt][:].rearrange("p (c i j) -> p c j i", i=4, j=PACK),
+                in_=w_raw[i][:, :, mt * P : (mt + 1) * P].rearrange("p j (c i) -> p c j i", i=4),
             )
-            return grouped
 
-        def quantize_w(i, grouped):
-            nc.vector.quantize_mx(out=w_codes[i][:].bitcast(FP8X4), scales=w_scales[i][:], in_=grouped[:])
+        def quantize_w(i, mt):
+            cols = slice(mt * P, (mt + 1) * P)
+            nc.vector.quantize_mx(out=w_codes[i][:, cols].bitcast(FP8X4), scales=w_scales[i][:, cols], in_=w_grouped[i, mt][:])
 
         def next_bank():
             return psum.tile([P, HALF], F32, name="acc", tag="acc", bufs=ACC_BANKS)
 
-        def by_feature(i, mt, h, scale, name):
+        def by_feature(i, mt, h, func, scale, name):
             acc = next_bank()
             value = fresh(name, HALF)
             nc.tensor.matmul_mx(
@@ -118,7 +123,7 @@ def tile_picked_highway_tanh_l_kernel(tc, xT, res, w1, w2, offs, out):
                 start=True,
                 stop=True,
             )
-            nc.scalar.activation(value, acc[:], ACT.Tanh, scale=scale)
+            nc.scalar.activation(value, acc[:], func, scale=scale)
             return value
 
         def gate_by_entry(mt, h, func, scale, name):
@@ -159,42 +164,48 @@ def tile_picked_highway_tanh_l_kernel(tc, xT, res, w1, w2, offs, out):
 
         gather_plane(0)
         gather_plane(1)
-        insert(0)
+        insert(0, 0)
+        insert(0, 1)
         gather_plane(2)
         gather_plane(3)
-        w1_grouped = group_w(LAYER)
-        w2_grouped = group_w(GATE)
-        quantize_x(direct[0], 0, PIECE)
-        quantize_x(direct[1], PIECE, HALF)
-        quantize_w(LAYER, w1_grouped)
-        insert(1)
-        x_codes[1] = keep.tile([P, HALF], U32, name="x_codes1", tag="w_grouped0", align_bytes=64)
-        quantize_x(woven, HALF, S)
-        quantize_w(GATE, w2_grouped)
+        group_w(nc.scalar.copy, LAYER, 0)
+        group_w(nc.scalar.copy, LAYER, 1)
+        group_w(nc.scalar.copy, GATE, 0)
+        insert(1, 0)
+        quantize_x(direct, 0, DIRECT)
+        quantize_x(woven[0], DIRECT, HALF)
+        insert(1, 1)
+        quantize_w(LAYER, 0)
+        x_codes[1] = keep.tile([P, HALF], U32, name="x_codes1", tag="w_grouped00", align_bytes=64)
+        quantize_x(woven[1], HALF, S)
+        quantize_w(LAYER, 1)
+        group_w(nc.vector.tensor_copy, GATE, 1)
+        quantize_w(GATE, 0)
+        quantize_w(GATE, 1)
 
         neg_y = {}
         gate = {}
-        neg_y[0, 0] = by_feature(LAYER, 0, 0, -1.0, "y00")
-        neg_y[0, 1] = by_feature(LAYER, 0, 1, -1.0, "y01")
-        gate[0, 0] = gate_by_entry(0, 0, ACT.Sigmoid, -1.0, "s00")
+        neg_y[0, 0] = by_feature(LAYER, 0, 0, ACT.Tanh, -1.0, "y00")
+        neg_y[0, 1] = by_feature(LAYER, 0, 1, ACT.Tanh, -1.0, "y01")
+        gate[0, 0] = by_feature(GATE, 0, 0, ACT.Sigmoid, -1.0, "s00")
         gate[0, 1] = gate_by_entry(0, 1, ACT.Sigmoid, -1.0, "s01")
-        neg_y[1, 1] = by_feature(LAYER, 1, 1, -1.0, "y11")
+        neg_y[1, 1] = by_feature(LAYER, 1, 1, ACT.Tanh, -1.0, "y11")
         gate[1, 1] = gate_by_entry(1, 1, ACT.Tanh, half[:], "t11")
-        neg_y[1, 0] = by_feature(LAYER, 1, 0, -1.0, "y10")
+        neg_y[1, 0] = by_feature(LAYER, 1, 0, ACT.Tanh, -1.0, "y10")
         gate[1, 0] = gate_by_entry(1, 0, ACT.Tanh, half[:], "t10")
 
         d = {}
-        s_back = {}
         for h in range(2):
             d[h] = fresh("d0%d" % h, HALF)
             nc.vector.tensor_tensor(d[h], res_rows[0][:].indirect(entries(h * HALF, (h + 1) * HALF)), neg_y[0, h], ALU.add)
-            s_back[h] = psum.tile([P, HALF], F32, name="s_back%d" % h, tag="side%d" % h)
-            turn(s_back[h], gate[0, h], HALF, True, True)
+        s_back = psum.tile([P, HALF], F32, name="s_back", tag="side0")
+        turn(s_back, gate[0, 1], HALF, True, True)
+        e = [fresh("e0%d" % h, HALF) for h in range(2)]
+        nc.gpsimd.tensor_tensor(e[0], gate[0, 0], d[0], ALU.mult)
+        nc.vector.tensor_tensor(e[1], s_back[:], d[1], ALU.mult)
         for h in range(2):
-            e = fresh("e0%d" % h, HALF)
-            nc.vector.tensor_tensor(e, s_back[h][:], d[h], ALU.mult)
             result = fresh("result0%d" % h, HALF)
-            nc.gpsimd.tensor_tensor(result, e, neg_y[0, h], ALU.subtract)
+            nc.gpsimd.tensor_tensor(result, e[h], neg_y[0, h], ALU.subtract)
             nc.sync.dma_start(out=out[0:P, h * HALF : (h + 1) * HALF], in_=result)
 
         def part(tiles, n):

@@ -111,24 +111,25 @@ def tile_picked_highway_tanh_l_kernel(tc, xT, res, w1, w2, offs, out):
         def next_bank():
             return psum.tile([P, HALF], F32, name="acc", tag="acc", bufs=ACC_BANKS)
 
-        def by_feature(i, mt, h, func, scale, name):
-            acc = next_bank()
+        def by_feature(i, mt, h, func, scale, name, width=HALF):
             value = fresh(name, HALF)
-            nc.tensor.matmul_mx(
-                out=acc[:],
-                lhsT=w_codes[i][:, mt * P : (mt + 1) * P].bitcast(FP8X4),
-                lhsT_scale=w_scales[i][:, mt * P : (mt + 1) * P],
-                rhs=x_codes[h][:].bitcast(FP8X4),
-                rhs_scale=x_scales[h][:],
-                start=True,
-                stop=True,
-            )
-            nc.scalar.activation(value, acc[:], func, scale=scale)
+            for a in range(0, HALF, width):
+                acc = next_bank()
+                cols = slice(a, a + width)
+                nc.tensor.matmul_mx(
+                    out=acc[:, 0:width],
+                    lhsT=w_codes[i][:, mt * P : (mt + 1) * P].bitcast(FP8X4),
+                    lhsT_scale=w_scales[i][:, mt * P : (mt + 1) * P],
+                    rhs=x_codes[h][:, cols].bitcast(FP8X4),
+                    rhs_scale=x_scales[h][:, cols],
+                    start=True,
+                    stop=True,
+                )
+                nc.scalar.activation(value[:, cols], acc[:, 0:width], func, scale=scale)
             return value
 
-        def gate_by_entry(mt, h, func, scale, name):
+        def gate_by_entry(mt, h):
             acc = next_bank()
-            value = fresh(name, HALF)
             for block in range(HALF // P):
                 cols = slice(block * P, (block + 1) * P)
                 nc.tensor.matmul_mx(
@@ -140,7 +141,11 @@ def tile_picked_highway_tanh_l_kernel(tc, xT, res, w1, w2, offs, out):
                     start=True,
                     stop=True,
                 )
-            nc.scalar.activation(value, acc[:], func, scale=scale)
+            return acc
+
+        def activate(acc, func, scale, value, width):
+            for a in range(0, HALF, width):
+                nc.scalar.activation(value[:, a : a + width], acc[:, a : a + width], func, scale=scale)
             return value
 
         def turn(bank, src, width, first, last):
@@ -185,21 +190,25 @@ def tile_picked_highway_tanh_l_kernel(tc, xT, res, w1, w2, offs, out):
 
         neg_y = {}
         gate = {}
-        neg_y[0, 0] = by_feature(LAYER, 0, 0, ACT.Tanh, -1.0, "y00")
+        neg_y[0, 0] = by_feature(LAYER, 0, 0, ACT.Tanh, -1.0, "y00", PIECE)
         neg_y[0, 1] = by_feature(LAYER, 0, 1, ACT.Tanh, -1.0, "y01")
+        gate[0, 1] = activate(gate_by_entry(0, 1), ACT.Sigmoid, -1.0, fresh("s01", HALF), HALF)
+        s_back = psum.tile([P, HALF], F32, name="s_back", tag="side0")
+        turn(s_back, gate[0, 1], HALF, True, True)
         gate[0, 0] = by_feature(GATE, 0, 0, ACT.Sigmoid, -1.0, "s00")
-        gate[0, 1] = gate_by_entry(0, 1, ACT.Sigmoid, -1.0, "s01")
         neg_y[1, 1] = by_feature(LAYER, 1, 1, ACT.Tanh, -1.0, "y11")
-        gate[1, 1] = gate_by_entry(1, 1, ACT.Tanh, half[:], "t11")
         neg_y[1, 0] = by_feature(LAYER, 1, 0, ACT.Tanh, -1.0, "y10")
-        gate[1, 0] = gate_by_entry(1, 0, ACT.Tanh, half[:], "t10")
+        gate[1, 1] = activate(gate_by_entry(1, 1), ACT.Tanh, half[:], fresh("t11", HALF), HALF)
+        acc10 = gate_by_entry(1, 0)
 
         d = {}
         for h in range(2):
             d[h] = fresh("d0%d" % h, HALF)
-            nc.vector.tensor_tensor(d[h], res_rows[0][:].indirect(entries(h * HALF, (h + 1) * HALF)), neg_y[0, h], ALU.add)
-        s_back = psum.tile([P, HALF], F32, name="s_back", tag="side0")
-        turn(s_back, gate[0, 1], HALF, True, True)
+            width = PIECE if h == 0 else HALF
+            for a in range(0, HALF, width):
+                cols = slice(a, a + width)
+                window = res_rows[0][:].indirect(entries(h * HALF + a, h * HALF + a + width))
+                nc.vector.tensor_tensor(d[h][:, cols], window, neg_y[0, h][:, cols], ALU.add)
         e = [fresh("e0%d" % h, HALF) for h in range(2)]
         nc.gpsimd.tensor_tensor(e[0], gate[0, 0], d[0], ALU.mult)
         nc.vector.tensor_tensor(e[1], s_back[:], d[1], ALU.mult)
@@ -229,6 +238,8 @@ def tile_picked_highway_tanh_l_kernel(tc, xT, res, w1, w2, offs, out):
             else:
                 nc.scalar.activation(r, window, ACT.Copy)
             turn(diff[n], r, PIECE, False, True)
+        gate[1, 0] = activate(acc10, ACT.Tanh, half[:], fresh("t10", HALF, tag="r1_2"), PIECE)
+        order = [2, 3, 0, 1]
         for place, n in enumerate(order):
             e_turned = weigh("e1_%d" % n, part(gate, n), diff[n][:, 0:PIECE], PIECE)
             if place < 2:

@@ -111,37 +111,24 @@ def tile_picked_highway_tanh_l_kernel(tc, xT, res, w1, w2, offs, out):
         def next_bank():
             return psum.tile([P, HALF], F32, name="acc", tag="acc", bufs=ACC_BANKS)
 
-        def by_feature(i, mt, h, func, scale, name, width=HALF):
-            value = fresh(name, HALF)
-            for a in range(0, HALF, width):
-                acc = next_bank()
-                cols = slice(a, a + width)
+        def product(acc, i, mt, a, b, by_entry):
+            h, o = divmod(a, HALF)
+            w_cols = slice(mt * P, (mt + 1) * P)
+            step = P if by_entry else b - a
+            for n in range(0, b - a, step):
+                x_cols = slice(o + n, o + n + step)
+                w_side = (w_codes[i][:, w_cols].bitcast(FP8X4), w_scales[i][:, w_cols])
+                x_side = (x_codes[h][:, x_cols].bitcast(FP8X4), x_scales[h][:, x_cols])
+                fixed, moving = (x_side, w_side) if by_entry else (w_side, x_side)
                 nc.tensor.matmul_mx(
-                    out=acc[:, 0:width],
-                    lhsT=w_codes[i][:, mt * P : (mt + 1) * P].bitcast(FP8X4),
-                    lhsT_scale=w_scales[i][:, mt * P : (mt + 1) * P],
-                    rhs=x_codes[h][:, cols].bitcast(FP8X4),
-                    rhs_scale=x_scales[h][:, cols],
+                    out=acc[:, n : n + step],
+                    lhsT=fixed[0],
+                    lhsT_scale=fixed[1],
+                    rhs=moving[0],
+                    rhs_scale=moving[1],
                     start=True,
                     stop=True,
                 )
-                nc.scalar.activation(value[:, cols], acc[:, 0:width], func, scale=scale)
-            return value
-
-        def gate_by_entry(mt, h):
-            acc = next_bank()
-            for block in range(HALF // P):
-                cols = slice(block * P, (block + 1) * P)
-                nc.tensor.matmul_mx(
-                    out=acc[:, cols],
-                    lhsT=x_codes[h][:, cols].bitcast(FP8X4),
-                    lhsT_scale=x_scales[h][:, cols],
-                    rhs=w_codes[GATE][:, mt * P : (mt + 1) * P].bitcast(FP8X4),
-                    rhs_scale=w_scales[GATE][:, mt * P : (mt + 1) * P],
-                    start=True,
-                    stop=True,
-                )
-            return acc
 
         def activate(acc, func, scale, value, width):
             for a in range(0, HALF, width):
@@ -156,16 +143,6 @@ def tile_picked_highway_tanh_l_kernel(tc, xT, res, w1, w2, offs, out):
                     bank[:, cols], src[:, cols], ident[:], is_transpose=True,
                     start=(first and block == 0), stop=(last and block == blocks - 1),
                 )
-
-        def weigh(name, t, d, width):
-            e = fresh(name, width)
-            nc.vector.scalar_tensor_tensor(out=e, in0=t, scalar=-1.0, in1=d, op0=ALU.add, op1=ALU.mult)
-            return e
-
-        def finish(mt, a, b, e, neg_y):
-            result = fresh("result%d_%d" % (mt, a), b - a)
-            nc.vector.scalar_tensor_tensor(out=result, in0=e, scalar=-0.5, in1=neg_y, op0=ALU.mult, op1=ALU.subtract)
-            nc.sync.dma_start(out=out[mt * P : (mt + 1) * P, a:b], in_=result)
 
         gather_plane(0)
         gather_plane(1)
@@ -188,64 +165,100 @@ def tile_picked_highway_tanh_l_kernel(tc, xT, res, w1, w2, offs, out):
         quantize_w(GATE, 0)
         quantize_w(GATE, 1)
 
-        neg_y = {}
-        gate = {}
-        neg_y[0, 0] = by_feature(LAYER, 0, 0, ACT.Tanh, -1.0, "y00", PIECE)
-        neg_y[0, 1] = by_feature(LAYER, 0, 1, ACT.Tanh, -1.0, "y01")
-        gate[0, 1] = activate(gate_by_entry(0, 1), ACT.Sigmoid, -1.0, fresh("s01", HALF), HALF)
-        s_back = psum.tile([P, HALF], F32, name="s_back", tag="side0")
-        turn(s_back, gate[0, 1], HALF, True, True)
-        gate[0, 0] = by_feature(GATE, 0, 0, ACT.Sigmoid, -1.0, "s00")
-        neg_y[1, 1] = by_feature(LAYER, 1, 1, ACT.Tanh, -1.0, "y11")
-        neg_y[1, 0] = by_feature(LAYER, 1, 0, ACT.Tanh, -1.0, "y10")
-        gate[1, 1] = activate(gate_by_entry(1, 1), ACT.Tanh, half[:], fresh("t11", HALF), HALF)
-        acc10 = gate_by_entry(1, 0)
+        neg_y = [fresh("neg_y%d" % mt, S) for mt in range(2)]
 
-        d = {}
-        for h in range(2):
-            d[h] = fresh("d0%d" % h, HALF)
-            width = PIECE if h == 0 else HALF
-            for a in range(0, HALF, width):
-                cols = slice(a, a + width)
-                window = res_rows[0][:].indirect(entries(h * HALF + a, h * HALF + a + width))
-                nc.vector.tensor_tensor(d[h][:, cols], window, neg_y[0, h][:, cols], ALU.add)
-        e = [fresh("e0%d" % h, HALF) for h in range(2)]
-        nc.gpsimd.tensor_tensor(e[0], gate[0, 0], d[0], ALU.mult)
-        nc.vector.tensor_tensor(e[1], s_back[:], d[1], ALU.mult)
-        for h in range(2):
-            result = fresh("result0%d" % h, HALF)
-            nc.gpsimd.tensor_tensor(result, e[h], neg_y[0, h], ALU.subtract)
-            nc.sync.dma_start(out=out[0:P, h * HALF : (h + 1) * HALF], in_=result)
+        def layer(mt, a, b):
+            acc = next_bank()
+            product(acc, LAYER, mt, a, b, False)
+            nc.scalar.activation(neg_y[mt][:, a:b], acc[:, 0 : b - a], ACT.Tanh, scale=-1.0)
 
-        def part(tiles, n):
-            h, o = divmod(n * PIECE, HALF)
-            return tiles[1, h][:, o : o + PIECE]
+        SPLIT = HALF + PIECE
+        layer(0, 0, PIECE)
+        layer(0, PIECE, HALF)
+        layer(0, HALF, S)
+        s_low = fresh("s_low", S)
+        acc = next_bank()
+        product(acc, GATE, 0, 0, HALF, False)
+        nc.scalar.activation(s_low[:, 0:HALF], acc[:], ACT.Sigmoid, scale=-1.0)
+        acc = next_bank()
+        product(acc[:, 0:PIECE], GATE, 0, HALF, SPLIT, False)
+        product(acc[:, PIECE:HALF], GATE, 0, SPLIT, S, True)
+        nc.scalar.activation(s_low[:, HALF:S], acc[:], ACT.Sigmoid, scale=-1.0)
+        layer(1, HALF, S)
+        layer(1, 0, HALF)
+        s11 = fresh("s11", HALF)
+        acc = next_bank()
+        product(acc, GATE, 1, HALF, S, True)
+        nc.scalar.activation(s11, acc[:], ACT.Sigmoid, scale=-1.0)
+        acc10 = next_bank()
+        product(acc10, GATE, 1, 0, HALF, True)
 
-        order = [2, 0, 3, 1]
+        d_low = fresh("d_low", SPLIT)
+        for a in range(0, SPLIT, PIECE):
+            cols = slice(a, a + PIECE)
+            nc.vector.tensor_tensor(d_low[:, cols], res_rows[0][:].indirect(entries(a, a + PIECE)), neg_y[0][:, cols], ALU.add)
+        for a, b in ((0, HALF), (HALF, SPLIT)):
+            e = fresh("e_low%d" % a, b - a)
+            nc.gpsimd.tensor_tensor(e, s_low[:, a:b], d_low[:, a:b], ALU.mult)
+            result = fresh("result_low%d" % a, b - a)
+            nc.gpsimd.tensor_tensor(result, e, neg_y[0][:, a:b], ALU.subtract)
+            nc.sync.dma_start(out=out[0:P, a:b], in_=result)
+
         diff = {}
         back = {}
-        for n in order:
-            if n >= 2:
-                diff[n] = psum.tile([P, HALF], F32, name="diff%d" % n)
-            else:
-                diff[n] = next_bank()
-            turn(diff[n], part(neg_y, n), PIECE, True, False)
-        for n in order:
-            r = fresh("r1_%d" % n, PIECE)
-            window = res_rows[1][:].indirect(entries(n * PIECE, (n + 1) * PIECE))
-            if n >= 2:
+
+        def open_difference(mt, a, bank):
+            diff[mt, a] = bank
+            turn(bank, neg_y[mt][:, a : a + PIECE], PIECE, True, False)
+
+        def close_difference(mt, a, on_vector):
+            r = fresh("r%d_%d" % (mt, a), PIECE)
+            window = res_rows[mt][:].indirect(entries(a, a + PIECE))
+            if on_vector:
                 nc.vector.tensor_copy(out=r, in_=window)
             else:
                 nc.scalar.activation(r, window, ACT.Copy)
-            turn(diff[n], r, PIECE, False, True)
-        gate[1, 0] = activate(acc10, ACT.Tanh, half[:], fresh("t10", HALF, tag="r1_2"), PIECE)
-        order = [2, 3, 0, 1]
-        for place, n in enumerate(order):
-            e_turned = weigh("e1_%d" % n, part(gate, n), diff[n][:, 0:PIECE], PIECE)
-            if place < 2:
-                back[n] = psum.tile([P, HALF], F32, name="back%d" % n, tag="side%d" % place)
+            turn(diff[mt, a], r, PIECE, False, True)
+
+        def weigh(mt, a, gate, e, bank):
+            if mt == 1 and a < HALF:
+                nc.vector.scalar_tensor_tensor(
+                    out=e, in0=gate, scalar=-1.0, in1=diff[mt, a][:, 0:PIECE], op0=ALU.add, op1=ALU.mult
+                )
             else:
-                back[n] = next_bank()
-            turn(back[n], e_turned, PIECE, True, True)
-        for n in order:
-            finish(1, n * PIECE, (n + 1) * PIECE, back[n][:, 0:PIECE], part(neg_y, n))
+                nc.vector.tensor_tensor(e, gate, diff[mt, a][:, 0:PIECE], ALU.mult)
+            back[mt, a] = bank
+            turn(bank, e, PIECE, True, True)
+
+        def finish(mt, a):
+            result = fresh("result%d_%d" % (mt, a), PIECE)
+            y = neg_y[mt][:, a : a + PIECE]
+            e = back[mt, a][:, 0:PIECE]
+            if mt == 1 and a < HALF:
+                nc.vector.scalar_tensor_tensor(out=result, in0=e, scalar=-0.5, in1=y, op0=ALU.mult, op1=ALU.subtract)
+            else:
+                nc.vector.scalar_tensor_tensor(out=result, in0=y, scalar=-1.0, in1=e, op0=ALU.mult, op1=ALU.add)
+            nc.sync.dma_start(out=out[mt * P : (mt + 1) * P, a : a + PIECE], in_=result)
+
+        open_difference(0, SPLIT, psum.tile([P, HALF], F32, name="diff_low", tag="side0"))
+        close_difference(0, SPLIT, True)
+        open_difference(1, HALF, psum.tile([P, HALF], F32, name="diff2", tag="diff2"))
+        open_difference(1, SPLIT, psum.tile([P, HALF], F32, name="diff3", tag="diff3"))
+        open_difference(1, 0, next_bank())
+        open_difference(1, PIECE, next_bank())
+        close_difference(1, HALF, True)
+        close_difference(1, SPLIT, True)
+        close_difference(1, 0, False)
+        close_difference(1, PIECE, False)
+        late = fresh("late", SPLIT, tag="r1_512")
+        t10 = activate(acc10, ACT.Tanh, half[:], late[:, 0:HALF], PIECE)
+        weigh(0, SPLIT, s_low[:, SPLIT:S], late[:, HALF:SPLIT], psum.tile([P, HALF], F32, name="back_low", tag="side1"))
+        weigh(1, HALF, s11[:, 0:PIECE], fresh("e1_2", PIECE), next_bank())
+        weigh(1, SPLIT, s11[:, PIECE:HALF], fresh("e1_3", PIECE), psum.tile([P, HALF], F32, name="back3", tag="side0"))
+        finish(0, SPLIT)
+        weigh(1, 0, t10[:, 0:PIECE], fresh("e1_0", PIECE), psum.tile([P, HALF], F32, name="back0", tag="diff2"))
+        weigh(1, PIECE, t10[:, PIECE:HALF], fresh("e1_1", PIECE), psum.tile([P, HALF], F32, name="back1", tag="diff3"))
+        finish(1, HALF)
+        finish(1, SPLIT)
+        finish(1, 0)
+        finish(1, PIECE)

@@ -211,13 +211,13 @@ def tile_picked_highway_tanh_l_kernel(tc, xT, res, w1, w2, offs, out):
             diff[mt, a] = bank
             turn(bank, neg_y[mt][:, a : a + PIECE], PIECE, True, False)
 
-        def close_difference(mt, a, on_vector):
+        def close_difference(mt, a, on_scalar):
             r = fresh("r%d_%d" % (mt, a), PIECE)
-            window = res_rows[mt][:].indirect(entries(a, a + PIECE))
-            if on_vector:
-                nc.vector.tensor_copy(out=r, in_=window)
-            else:
-                nc.scalar.activation(r, window, ACT.Copy)
+            if on_scalar < PIECE:
+                window = res_rows[mt][:].indirect(entries(a + on_scalar, a + PIECE))
+                nc.vector.tensor_copy(out=r[:, on_scalar:PIECE], in_=window)
+            if on_scalar > 0:
+                nc.scalar.activation(r[:, 0:on_scalar], res_rows[mt][:].indirect(entries(a, a + on_scalar)), ACT.Copy)
             turn(diff[mt, a], r, PIECE, False, True)
 
         def weigh(mt, a, gate, e, bank):
@@ -241,15 +241,15 @@ def tile_picked_highway_tanh_l_kernel(tc, xT, res, w1, w2, offs, out):
             nc.sync.dma_start(out=out[mt * P : (mt + 1) * P, a : a + PIECE], in_=result)
 
         open_difference(0, SPLIT, psum.tile([P, HALF], F32, name="diff_low", tag="side0"))
-        close_difference(0, SPLIT, True)
+        close_difference(0, SPLIT, 0)
         open_difference(1, HALF, psum.tile([P, HALF], F32, name="diff2", tag="diff2"))
         open_difference(1, SPLIT, psum.tile([P, HALF], F32, name="diff3", tag="diff3"))
         open_difference(1, 0, next_bank())
         open_difference(1, PIECE, next_bank())
-        close_difference(1, HALF, True)
-        close_difference(1, SPLIT, True)
-        close_difference(1, 0, False)
-        close_difference(1, PIECE, False)
+        close_difference(1, HALF, 0)
+        close_difference(1, SPLIT, 0)
+        close_difference(1, 0, PIECE)
+        close_difference(1, PIECE, P)
         late = fresh("late", SPLIT, tag="r1_512")
         t10 = activate(acc10, ACT.Tanh, half[:], late[:, 0:HALF], PIECE)
         weigh(0, SPLIT, s_low[:, SPLIT:S], late[:, HALF:SPLIT], psum.tile([P, HALF], F32, name="back_low", tag="side1"))

@@ -20,9 +20,10 @@ PACK = 4
 LIST_ROWS = 16
 HALF = 512
 PIECE = 256
+ON_GPSIMD = HALF + PIECE
 ACC_BANKS = 4
 LAYER, GATE = 0, 1
-DIRECT = 384
+LOW, HIGH = 0, 1
 
 
 def tile_picked_highway_tanh_l_kernel(tc, xT, res, w1, w2, offs, out):
@@ -47,8 +48,8 @@ def tile_picked_highway_tanh_l_kernel(tc, xT, res, w1, w2, offs, out):
 
         zero = keep.tile([P, 1], F32, name="zero")
         nc.gpsimd.memset(zero[:], 0.0)
-        half = keep.tile([P, 1], F32, name="half")
-        nc.scalar.activation(half[:], zero[:], ACT.Sigmoid)
+        one_half = keep.tile([P, 1], F32, name="one_half")
+        nc.scalar.activation(one_half[:], zero[:], ACT.Sigmoid)
 
         planes = []
         for j in range(PACK):
@@ -62,64 +63,94 @@ def tile_picked_highway_tanh_l_kernel(tc, xT, res, w1, w2, offs, out):
             raw = keep.tile([P, PACK, N], F32, name="w_raw%d" % i, align_bytes=64)
             nc.sync.dma_start(out=raw[:], in_=w.rearrange("(p j) n -> p j n", j=PACK))
             w_raw.append(raw)
-        res_rows = [keep.tile([P, T], F32, name="res%d" % mt) for mt in range(2)]
-        for mt in range(2):
-            nc.sync.dma_start(out=res_rows[mt][:], in_=res[mt * P : (mt + 1) * P, :])
+        res_rows = [keep.tile([P, T], F32, name="res%d" % rows) for rows in (LOW, HIGH)]
+        for rows in (LOW, HIGH):
+            nc.sync.dma_start(out=res_rows[rows][:], in_=res[rows * P : (rows + 1) * P, :])
 
-        direct = keep.tile([P, DIRECT, PACK], BF16, name="direct", align_bytes=64)
-        spans = [(DIRECT, HALF), (HALF, S)]
-        woven = [keep.tile([P, b - a, PACK], BF16, name="woven%d" % a, align_bytes=64) for a, b in spans]
+        starts = range(0, S, PIECE)
+        on_scalar = starts[1:]
+        woven = {a: keep.tile([P, PIECE, PACK], BF16, name="woven%d" % a, align_bytes=64) for a in starts}
         flat = [
-            [keep.tile([P, 2, b - a], BF16, name="flat%d_%d" % (u, a), align_bytes=64) for a, b in spans]
+            {a: keep.tile([P, 2, PIECE], BF16, name="flat%d_%d" % (u, a), align_bytes=64) for a in on_scalar}
             for u in range(2)
         ]
-        x_codes = {0: keep.tile([P, HALF], U32, name="x_codes0", align_bytes=64)}
+        x_codes = [keep.tile([P, HALF], U32, name="x_codes0", align_bytes=64)]
         x_scales = [keep.tile([P, HALF], U8, name="x_scales%d" % h, align_bytes=64) for h in range(2)]
 
         def gather_plane(j):
-            nc.vector.tensor_copy(out=direct[:, :, j], in_=planes[j][:].indirect(entries(0, DIRECT)))
-            for n, (a, b) in enumerate(spans):
-                nc.scalar.activation(flat[j // 2][n][:, j % 2, :], planes[j][:].indirect(entries(a, b)), ACT.Copy)
+            nc.vector.tensor_copy(out=woven[0][:, :, j], in_=planes[j][:].indirect(entries(0, PIECE)))
+            for a in on_scalar:
+                nc.scalar.activation(
+                    flat[j // 2][a][:, j % 2, :], planes[j][:].indirect(entries(a, a + PIECE)), ACT.Copy
+                )
 
-        def insert(u, n):
-            nc.vector.tensor_copy(out=woven[n][:, :, 2 * u : 2 * u + 2], in_=flat[u][n][:].rearrange("p j n -> p n j"))
+        def insert(u, a):
+            nc.vector.tensor_copy(out=woven[a][:, :, 2 * u : 2 * u + 2], in_=flat[u][a][:].rearrange("p i n -> p n i"))
 
-        def quantize_x(src, a, b):
+        def quantize_x(a):
             h, o = divmod(a, HALF)
             nc.vector.quantize_mx(
-                out=x_codes[h][:, o : o + b - a].bitcast(FP8X4),
-                scales=x_scales[h][:, o : o + b - a],
-                in_=src[:].rearrange("p n j -> p (n j)"),
+                out=x_codes[h][:, o : o + PIECE].bitcast(FP8X4),
+                scales=x_scales[h][:, o : o + PIECE],
+                in_=woven[a][:].rearrange("p n j -> p (n j)"),
             )
 
-        w_codes = [keep.tile([P, N], U32, name="w_codes%d" % i, align_bytes=64) for i in range(2)]
-        w_scales = [keep.tile([P, N], U8, name="w_scales%d" % i, align_bytes=64) for i in range(2)]
-        w_grouped = {}
+        w_codes = [keep.tile([P, N], U32, name="w_codes%d" % i, align_bytes=64) for i in (LAYER, GATE)]
+        w_scales = [keep.tile([P, N], U8, name="w_scales%d" % i, align_bytes=64) for i in (LAYER, GATE)]
+        w_woven = {}
 
-        def group_w(copy, i, mt):
-            name = "w_grouped%d%d" % (i, mt)
-            w_grouped[i, mt] = keep.tile([P, P * PACK], BF16, name=name, tag=name, align_bytes=64)
+        def weave_w(copy, i, rows):
+            name = "w_woven%d%d" % (i, rows)
+            w_woven[i, rows] = keep.tile([P, P * PACK], BF16, name=name, tag=name, align_bytes=64)
             copy(
-                out=w_grouped[i, mt][:].rearrange("p (c i j) -> p c j i", i=4, j=PACK),
-                in_=w_raw[i][:, :, mt * P : (mt + 1) * P].rearrange("p j (c i) -> p c j i", i=4),
+                out=w_woven[i, rows][:].rearrange("p (c n j) -> p c j n", n=4, j=PACK),
+                in_=w_raw[i][:, :, rows * P : (rows + 1) * P].rearrange("p j (c n) -> p c j n", n=4),
             )
 
-        def quantize_w(i, mt):
-            cols = slice(mt * P, (mt + 1) * P)
-            nc.vector.quantize_mx(out=w_codes[i][:, cols].bitcast(FP8X4), scales=w_scales[i][:, cols], in_=w_grouped[i, mt][:])
+        def quantize_w(i, rows):
+            cols = slice(rows * P, (rows + 1) * P)
+            nc.vector.quantize_mx(
+                out=w_codes[i][:, cols].bitcast(FP8X4), scales=w_scales[i][:, cols], in_=w_woven[i, rows][:]
+            )
+
+        gather_plane(0)
+        gather_plane(1)
+        for a in on_scalar:
+            insert(0, a)
+        gather_plane(2)
+        gather_plane(3)
+        weave_w(nc.scalar.copy, LAYER, LOW)
+        weave_w(nc.scalar.copy, LAYER, HIGH)
+        weave_w(nc.scalar.copy, GATE, LOW)
+        insert(1, PIECE)
+        quantize_x(0)
+        quantize_x(PIECE)
+        insert(1, HALF)
+        insert(1, HALF + PIECE)
+        quantize_w(LAYER, LOW)
+        x_codes.append(keep.tile([P, HALF], U32, name="x_codes1", tag="w_woven00", align_bytes=64))
+        quantize_x(HALF)
+        quantize_x(HALF + PIECE)
+        quantize_w(LAYER, HIGH)
+        weave_w(nc.vector.tensor_copy, GATE, HIGH)
+        quantize_w(GATE, LOW)
+        quantize_w(GATE, HIGH)
 
         def next_bank():
             return psum.tile([P, HALF], F32, name="acc", tag="acc", bufs=ACC_BANKS)
 
-        def product(acc, i, mt, a, b, by_entry):
+        def own_bank(name, tag):
+            return psum.tile([P, HALF], F32, name=name, tag=tag)
+
+        def product(acc, i, rows, a, b, turned):
             h, o = divmod(a, HALF)
-            w_cols = slice(mt * P, (mt + 1) * P)
-            step = P if by_entry else b - a
+            w_cols = slice(rows * P, (rows + 1) * P)
+            step = P if turned else b - a
             for n in range(0, b - a, step):
                 x_cols = slice(o + n, o + n + step)
                 w_side = (w_codes[i][:, w_cols].bitcast(FP8X4), w_scales[i][:, w_cols])
                 x_side = (x_codes[h][:, x_cols].bitcast(FP8X4), x_scales[h][:, x_cols])
-                fixed, moving = (x_side, w_side) if by_entry else (w_side, x_side)
+                fixed, moving = (x_side, w_side) if turned else (w_side, x_side)
                 nc.tensor.matmul_mx(
                     out=acc[:, n : n + step],
                     lhsT=fixed[0],
@@ -130,13 +161,48 @@ def tile_picked_highway_tanh_l_kernel(tc, xT, res, w1, w2, offs, out):
                     stop=True,
                 )
 
-        def activate(acc, func, scale, value, width):
-            for a in range(0, HALF, width):
-                nc.scalar.activation(value[:, a : a + width], acc[:, a : a + width], func, scale=scale)
-            return value
+        neg_y = [fresh("neg_y%d" % rows, S) for rows in (LOW, HIGH)]
 
-        def turn(bank, src, width, first, last):
-            blocks = width // P
+        def layer(rows, a, b):
+            acc = next_bank()
+            product(acc, LAYER, rows, a, b, False)
+            nc.scalar.activation(neg_y[rows][:, a:b], acc[:, 0 : b - a], ACT.Tanh, scale=-1.0)
+
+        layer(LOW, 0, PIECE)
+        layer(LOW, PIECE, HALF)
+        layer(LOW, HALF, S)
+        s_low = fresh("s_low", S)
+        acc = next_bank()
+        product(acc, GATE, LOW, 0, HALF, False)
+        nc.scalar.activation(s_low[:, 0:HALF], acc[:], ACT.Sigmoid, scale=-1.0)
+        acc = next_bank()
+        product(acc[:, 0:PIECE], GATE, LOW, HALF, ON_GPSIMD, False)
+        product(acc[:, PIECE:HALF], GATE, LOW, ON_GPSIMD, S, True)
+        nc.scalar.activation(s_low[:, HALF:S], acc[:], ACT.Sigmoid, scale=-1.0)
+        layer(HIGH, HALF, S)
+        layer(HIGH, 0, HALF)
+        s_high = fresh("s_high", HALF)
+        acc = next_bank()
+        product(acc, GATE, HIGH, HALF, S, True)
+        nc.scalar.activation(s_high, acc[:], ACT.Sigmoid, scale=-1.0)
+        last_gate = next_bank()
+        product(last_gate, GATE, HIGH, 0, HALF, True)
+
+        d_low = fresh("d_low", ON_GPSIMD)
+        for a in range(0, ON_GPSIMD, PIECE):
+            cols = slice(a, a + PIECE)
+            nc.vector.tensor_tensor(
+                d_low[:, cols], res_rows[LOW][:].indirect(entries(a, a + PIECE)), neg_y[LOW][:, cols], ALU.add
+            )
+        for a, b in ((0, HALF), (HALF, ON_GPSIMD)):
+            weighed = fresh("weighed_low%d" % a, b - a)
+            nc.gpsimd.tensor_tensor(weighed, s_low[:, a:b], d_low[:, a:b], ALU.mult)
+            result = fresh("result_low%d" % a, b - a)
+            nc.gpsimd.tensor_tensor(result, weighed, neg_y[LOW][:, a:b], ALU.subtract)
+            nc.sync.dma_start(out=out[0:P, a:b], in_=result)
+
+        def turn(bank, src, first, last):
+            blocks = PIECE // P
             for block in range(blocks):
                 cols = slice(block * P, (block + 1) * P)
                 nc.tensor.matmul(
@@ -144,121 +210,78 @@ def tile_picked_highway_tanh_l_kernel(tc, xT, res, w1, w2, offs, out):
                     start=(first and block == 0), stop=(last and block == blocks - 1),
                 )
 
-        gather_plane(0)
-        gather_plane(1)
-        insert(0, 0)
-        insert(0, 1)
-        gather_plane(2)
-        gather_plane(3)
-        group_w(nc.scalar.copy, LAYER, 0)
-        group_w(nc.scalar.copy, LAYER, 1)
-        group_w(nc.scalar.copy, GATE, 0)
-        insert(1, 0)
-        quantize_x(direct, 0, DIRECT)
-        quantize_x(woven[0], DIRECT, HALF)
-        insert(1, 1)
-        quantize_w(LAYER, 0)
-        x_codes[1] = keep.tile([P, HALF], U32, name="x_codes1", tag="w_grouped00", align_bytes=64)
-        quantize_x(woven[1], HALF, S)
-        quantize_w(LAYER, 1)
-        group_w(nc.vector.tensor_copy, GATE, 1)
-        quantize_w(GATE, 0)
-        quantize_w(GATE, 1)
-
-        neg_y = [fresh("neg_y%d" % mt, S) for mt in range(2)]
-
-        def layer(mt, a, b):
-            acc = next_bank()
-            product(acc, LAYER, mt, a, b, False)
-            nc.scalar.activation(neg_y[mt][:, a:b], acc[:, 0 : b - a], ACT.Tanh, scale=-1.0)
-
-        SPLIT = HALF + PIECE
-        layer(0, 0, PIECE)
-        layer(0, PIECE, HALF)
-        layer(0, HALF, S)
-        s_low = fresh("s_low", S)
-        acc = next_bank()
-        product(acc, GATE, 0, 0, HALF, False)
-        nc.scalar.activation(s_low[:, 0:HALF], acc[:], ACT.Sigmoid, scale=-1.0)
-        acc = next_bank()
-        product(acc[:, 0:PIECE], GATE, 0, HALF, SPLIT, False)
-        product(acc[:, PIECE:HALF], GATE, 0, SPLIT, S, True)
-        nc.scalar.activation(s_low[:, HALF:S], acc[:], ACT.Sigmoid, scale=-1.0)
-        layer(1, HALF, S)
-        layer(1, 0, HALF)
-        s11 = fresh("s11", HALF)
-        acc = next_bank()
-        product(acc, GATE, 1, HALF, S, True)
-        nc.scalar.activation(s11, acc[:], ACT.Sigmoid, scale=-1.0)
-        acc10 = next_bank()
-        product(acc10, GATE, 1, 0, HALF, True)
-
-        d_low = fresh("d_low", SPLIT)
-        for a in range(0, SPLIT, PIECE):
-            cols = slice(a, a + PIECE)
-            nc.vector.tensor_tensor(d_low[:, cols], res_rows[0][:].indirect(entries(a, a + PIECE)), neg_y[0][:, cols], ALU.add)
-        for a, b in ((0, HALF), (HALF, SPLIT)):
-            e = fresh("e_low%d" % a, b - a)
-            nc.gpsimd.tensor_tensor(e, s_low[:, a:b], d_low[:, a:b], ALU.mult)
-            result = fresh("result_low%d" % a, b - a)
-            nc.gpsimd.tensor_tensor(result, e, neg_y[0][:, a:b], ALU.subtract)
-            nc.sync.dma_start(out=out[0:P, a:b], in_=result)
-
         diff = {}
         back = {}
 
-        def open_difference(mt, a, bank):
-            diff[mt, a] = bank
-            turn(bank, neg_y[mt][:, a : a + PIECE], PIECE, True, False)
+        def open_difference(rows, a, bank):
+            diff[rows, a] = bank
+            turn(bank, neg_y[rows][:, a : a + PIECE], True, False)
 
-        def close_difference(mt, a, on_scalar):
-            r = fresh("r%d_%d" % (mt, a), PIECE)
-            if on_scalar < PIECE:
-                window = res_rows[mt][:].indirect(entries(a + on_scalar, a + PIECE))
-                nc.vector.tensor_copy(out=r[:, on_scalar:PIECE], in_=window)
-            if on_scalar > 0:
-                nc.scalar.activation(r[:, 0:on_scalar], res_rows[mt][:].indirect(entries(a, a + on_scalar)), ACT.Copy)
-            turn(diff[mt, a], r, PIECE, False, True)
+        def close_difference(rows, a, scalar_share):
+            r = fresh("r%d_%d" % (rows, a), PIECE)
+            if scalar_share < PIECE:
+                window = res_rows[rows][:].indirect(entries(a + scalar_share, a + PIECE))
+                nc.vector.tensor_copy(out=r[:, scalar_share:PIECE], in_=window)
+            if scalar_share > 0:
+                window = res_rows[rows][:].indirect(entries(a, a + scalar_share))
+                nc.scalar.activation(r[:, 0:scalar_share], window, ACT.Copy)
+            turn(diff[rows, a], r, False, True)
 
-        def weigh(mt, a, gate, e, bank):
-            if mt == 1 and a < HALF:
-                nc.vector.scalar_tensor_tensor(
-                    out=e, in0=gate, scalar=-1.0, in1=diff[mt, a][:, 0:PIECE], op0=ALU.add, op1=ALU.mult
-                )
-            else:
-                nc.vector.tensor_tensor(e, gate, diff[mt, a][:, 0:PIECE], ALU.mult)
-            back[mt, a] = bank
-            turn(bank, e, PIECE, True, True)
+        def store(rows, a, result):
+            nc.sync.dma_start(out=out[rows * P : (rows + 1) * P, a : a + PIECE], in_=result)
 
-        def finish(mt, a):
-            result = fresh("result%d_%d" % (mt, a), PIECE)
-            y = neg_y[mt][:, a : a + PIECE]
-            e = back[mt, a][:, 0:PIECE]
-            if mt == 1 and a < HALF:
-                nc.vector.scalar_tensor_tensor(out=result, in0=e, scalar=-0.5, in1=y, op0=ALU.mult, op1=ALU.subtract)
-            else:
-                nc.vector.scalar_tensor_tensor(out=result, in0=y, scalar=-1.0, in1=e, op0=ALU.mult, op1=ALU.add)
-            nc.sync.dma_start(out=out[mt * P : (mt + 1) * P, a : a + PIECE], in_=result)
+        def weigh_by_s(rows, a, s, weighed, bank):
+            nc.vector.tensor_tensor(weighed, s, diff[rows, a][:, 0:PIECE], ALU.mult)
+            back[rows, a] = bank
+            turn(bank, weighed, True, True)
 
-        open_difference(0, SPLIT, psum.tile([P, HALF], F32, name="diff_low", tag="side0"))
-        close_difference(0, SPLIT, 0)
-        open_difference(1, HALF, psum.tile([P, HALF], F32, name="diff2", tag="diff2"))
-        open_difference(1, SPLIT, psum.tile([P, HALF], F32, name="diff3", tag="diff3"))
-        open_difference(1, 0, next_bank())
-        open_difference(1, PIECE, next_bank())
-        close_difference(1, HALF, 0)
-        close_difference(1, SPLIT, 0)
-        close_difference(1, 0, PIECE)
-        close_difference(1, PIECE, P)
-        late = fresh("late", SPLIT, tag="r1_512")
-        t10 = activate(acc10, ACT.Tanh, half[:], late[:, 0:HALF], PIECE)
-        weigh(0, SPLIT, s_low[:, SPLIT:S], late[:, HALF:SPLIT], psum.tile([P, HALF], F32, name="back_low", tag="side1"))
-        weigh(1, HALF, s11[:, 0:PIECE], fresh("e1_2", PIECE), next_bank())
-        weigh(1, SPLIT, s11[:, PIECE:HALF], fresh("e1_3", PIECE), psum.tile([P, HALF], F32, name="back3", tag="side0"))
-        finish(0, SPLIT)
-        weigh(1, 0, t10[:, 0:PIECE], fresh("e1_0", PIECE), psum.tile([P, HALF], F32, name="back0", tag="diff2"))
-        weigh(1, PIECE, t10[:, PIECE:HALF], fresh("e1_1", PIECE), psum.tile([P, HALF], F32, name="back1", tag="diff3"))
-        finish(1, HALF)
-        finish(1, SPLIT)
-        finish(1, 0)
-        finish(1, PIECE)
+        def finish_by_s(rows, a):
+            result = fresh("result%d_%d" % (rows, a), PIECE)
+            nc.vector.scalar_tensor_tensor(
+                out=result, in0=neg_y[rows][:, a : a + PIECE], scalar=-1.0, in1=back[rows, a][:, 0:PIECE],
+                op0=ALU.mult, op1=ALU.add,
+            )
+            store(rows, a, result)
+
+        def weigh_by_t(rows, a, t, weighed, bank):
+            nc.vector.scalar_tensor_tensor(
+                out=weighed, in0=t, scalar=-1.0, in1=diff[rows, a][:, 0:PIECE], op0=ALU.add, op1=ALU.mult
+            )
+            back[rows, a] = bank
+            turn(bank, weighed, True, True)
+
+        def finish_by_t(rows, a):
+            result = fresh("result%d_%d" % (rows, a), PIECE)
+            nc.vector.scalar_tensor_tensor(
+                out=result, in0=back[rows, a][:, 0:PIECE], scalar=-0.5, in1=neg_y[rows][:, a : a + PIECE],
+                op0=ALU.mult, op1=ALU.subtract,
+            )
+            store(rows, a, result)
+
+        open_difference(LOW, ON_GPSIMD, own_bank("diff_low", "bank_a"))
+        close_difference(LOW, ON_GPSIMD, 0)
+        open_difference(HIGH, HALF, own_bank("diff_high2", "bank_c"))
+        open_difference(HIGH, HALF + PIECE, own_bank("diff_high3", "bank_d"))
+        open_difference(HIGH, 0, next_bank())
+        open_difference(HIGH, PIECE, next_bank())
+        close_difference(HIGH, HALF, 0)
+        close_difference(HIGH, HALF + PIECE, 0)
+        close_difference(HIGH, 0, PIECE)
+        close_difference(HIGH, PIECE, P)
+
+        late = fresh("late", HALF + PIECE, tag="r%d_%d" % (HIGH, HALF))
+        t_high = late[:, 0:HALF]
+        for a in range(0, HALF, PIECE):
+            cols = slice(a, a + PIECE)
+            nc.scalar.activation(t_high[:, cols], last_gate[:, cols], ACT.Tanh, scale=one_half[:])
+
+        weigh_by_s(LOW, ON_GPSIMD, s_low[:, ON_GPSIMD:S], late[:, HALF:], own_bank("back_low", "bank_b"))
+        weigh_by_s(HIGH, HALF, s_high[:, 0:PIECE], fresh("weighed2", PIECE), next_bank())
+        weigh_by_s(HIGH, HALF + PIECE, s_high[:, PIECE:HALF], fresh("weighed3", PIECE), own_bank("back3", "bank_a"))
+        finish_by_s(LOW, ON_GPSIMD)
+        weigh_by_t(HIGH, 0, t_high[:, 0:PIECE], fresh("weighed0", PIECE), own_bank("back0", "bank_c"))
+        weigh_by_t(HIGH, PIECE, t_high[:, PIECE:HALF], fresh("weighed1", PIECE), own_bank("back1", "bank_d"))
+        finish_by_s(HIGH, HALF)
+        finish_by_s(HIGH, HALF + PIECE)
+        finish_by_t(HIGH, 0)
+        finish_by_t(HIGH, PIECE)

from contextlib import ExitStack

import concourse.mybir as mybir
from concourse.masks import make_identity

K, T, S, N = 512, 2048, 1024, 256
FLOPS = 2 * 2 * K * N * S

F32 = mybir.dt.float32
BF16 = mybir.dt.bfloat16
U32 = mybir.dt.uint32
U16 = mybir.dt.uint16
U8 = mybir.dt.uint8
FP8X4 = mybir.dt.float8_e4m3fn_x4
ACT = mybir.ActivationFunctionType
ALU = mybir.AluOpType

P = 128
PACK = 4
LIST_ROWS = 16
HALF = 512
PIECE = 256
ON_GPSIMD = HALF + PIECE
ACC_BANKS = 4
LAYER, GATE = 0, 1
LOW, HIGH = 0, 1


def tile_picked_highway_tanh_l_kernel(tc, xT, res, w1, w2, offs, out):
    nc = tc.nc
    x_rows = xT.rearrange("(p j) t -> p j t", j=PACK)

    with ExitStack() as ctx:
        keep = ctx.enter_context(tc.tile_pool(name="keep", bufs=1))
        psum = ctx.enter_context(tc.psum_pool(name="psum", bufs=1))

        offsets = keep.tile([P, S // LIST_ROWS], U16, name="offsets")

        def entries(a, b):
            return offsets[:, a // LIST_ROWS : b // LIST_ROWS]

        def fresh(name, width, tag=None):
            tile = keep.tile([P, width], F32, name=name, tag=tag or name)
            return tile[:]

        ident = keep.tile([P, P], F32, name="ident")
        make_identity(nc, ident[:])

        zero = keep.tile([P, 1], F32, name="zero")
        nc.gpsimd.memset(zero[:], 0.0)
        one_half = keep.tile([P, 1], F32, name="one_half")
        nc.scalar.activation(one_half[:], zero[:], ACT.Sigmoid)

        planes = []
        for j in range(PACK):
            plane = keep.tile([P, T], F32, name="plane%d" % j)
            nc.sync.dma_start(out=plane[:], in_=x_rows[:, j, :])
            planes.append(plane)
            if j == 0:
                nc.sync.dma_start(offsets[:], offs)
        w_raw = []
        for i, w in enumerate((w1, w2)):
            raw = keep.tile([P, PACK, N], F32, name="w_raw%d" % i, align_bytes=64)
            nc.sync.dma_start(out=raw[:], in_=w.rearrange("(p j) n -> p j n", j=PACK))
            w_raw.append(raw)
        res_rows = [keep.tile([P, T], F32, name="res%d" % rows) for rows in (LOW, HIGH)]
        for rows in (LOW, HIGH):
            nc.sync.dma_start(out=res_rows[rows][:], in_=res[rows * P : (rows + 1) * P, :])

        starts = range(0, S, PIECE)
        on_scalar = starts[1:]
        woven = {a: keep.tile([P, PIECE, PACK], BF16, name="woven%d" % a, align_bytes=64) for a in starts}
        flat = [
            {a: keep.tile([P, 2, PIECE], BF16, name="flat%d_%d" % (u, a), align_bytes=64) for a in on_scalar}
            for u in range(2)
        ]
        x_codes = [keep.tile([P, HALF], U32, name="x_codes0", align_bytes=64)]
        x_scales = [keep.tile([P, HALF], U8, name="x_scales%d" % h, align_bytes=64) for h in range(2)]

        def gather_plane(j):
            nc.vector.tensor_copy(out=woven[0][:, :, j], in_=planes[j][:].indirect(entries(0, PIECE)))
            for a in on_scalar:
                nc.scalar.activation(
                    flat[j // 2][a][:, j % 2, :], planes[j][:].indirect(entries(a, a + PIECE)), ACT.Copy
                )

        def insert(u, a):
            nc.vector.tensor_copy(out=woven[a][:, :, 2 * u : 2 * u + 2], in_=flat[u][a][:].rearrange("p i n -> p n i"))

        def quantize_x(a):
            h, o = divmod(a, HALF)
            nc.vector.quantize_mx(
                out=x_codes[h][:, o : o + PIECE].bitcast(FP8X4),
                scales=x_scales[h][:, o : o + PIECE],
                in_=woven[a][:].rearrange("p n j -> p (n j)"),
            )

        w_codes = [keep.tile([P, N], U32, name="w_codes%d" % i, align_bytes=64) for i in (LAYER, GATE)]
        w_scales = [keep.tile([P, N], U8, name="w_scales%d" % i, align_bytes=64) for i in (LAYER, GATE)]
        w_woven = {}

        def weave_w(copy, i, rows):
            name = "w_woven%d%d" % (i, rows)
            w_woven[i, rows] = keep.tile([P, P * PACK], BF16, name=name, tag=name, align_bytes=64)
            copy(
                out=w_woven[i, rows][:].rearrange("p (c n j) -> p c j n", n=4, j=PACK),
                in_=w_raw[i][:, :, rows * P : (rows + 1) * P].rearrange("p j (c n) -> p c j n", n=4),
            )

        def quantize_w(i, rows):
            cols = slice(rows * P, (rows + 1) * P)
            nc.vector.quantize_mx(
                out=w_codes[i][:, cols].bitcast(FP8X4), scales=w_scales[i][:, cols], in_=w_woven[i, rows][:]
            )

        gather_plane(0)
        gather_plane(1)
        for a in on_scalar:
            insert(0, a)
        gather_plane(2)
        gather_plane(3)
        weave_w(nc.scalar.copy, LAYER, LOW)
        weave_w(nc.scalar.copy, LAYER, HIGH)
        weave_w(nc.scalar.copy, GATE, LOW)
        insert(1, PIECE)
        quantize_x(0)
        quantize_x(PIECE)
        insert(1, HALF)
        insert(1, HALF + PIECE)
        quantize_w(LAYER, LOW)
        x_codes.append(keep.tile([P, HALF], U32, name="x_codes1", tag="w_woven00", align_bytes=64))
        quantize_x(HALF)
        quantize_x(HALF + PIECE)
        quantize_w(LAYER, HIGH)
        weave_w(nc.vector.tensor_copy, GATE, HIGH)
        quantize_w(GATE, LOW)
        quantize_w(GATE, HIGH)

        def next_bank():
            return psum.tile([P, HALF], F32, name="acc", tag="acc", bufs=ACC_BANKS)

        def own_bank(name, tag):
            return psum.tile([P, HALF], F32, name=name, tag=tag)

        def product(acc, i, rows, a, b, turned):
            h, o = divmod(a, HALF)
            w_cols = slice(rows * P, (rows + 1) * P)
            step = P if turned else b - a
            for n in range(0, b - a, step):
                x_cols = slice(o + n, o + n + step)
                w_side = (w_codes[i][:, w_cols].bitcast(FP8X4), w_scales[i][:, w_cols])
                x_side = (x_codes[h][:, x_cols].bitcast(FP8X4), x_scales[h][:, x_cols])
                fixed, moving = (x_side, w_side) if turned else (w_side, x_side)
                nc.tensor.matmul_mx(
                    out=acc[:, n : n + step],
                    lhsT=fixed[0],
                    lhsT_scale=fixed[1],
                    rhs=moving[0],
                    rhs_scale=moving[1],
                    start=True,
                    stop=True,
                )

        neg_y = [fresh("neg_y%d" % rows, S) for rows in (LOW, HIGH)]

        def layer(rows, a, b):
            acc = next_bank()
            product(acc, LAYER, rows, a, b, False)
            nc.scalar.activation(neg_y[rows][:, a:b], acc[:, 0 : b - a], ACT.Tanh, scale=-1.0)

        layer(LOW, 0, PIECE)
        layer(LOW, PIECE, HALF)
        layer(LOW, HALF, S)
        s_low = fresh("s_low", S)
        acc = next_bank()
        product(acc, GATE, LOW, 0, HALF, False)
        nc.scalar.activation(s_low[:, 0:HALF], acc[:], ACT.Sigmoid, scale=-1.0)
        acc = next_bank()
        product(acc[:, 0:PIECE], GATE, LOW, HALF, ON_GPSIMD, False)
        product(acc[:, PIECE:HALF], GATE, LOW, ON_GPSIMD, S, True)
        nc.scalar.activation(s_low[:, HALF:S], acc[:], ACT.Sigmoid, scale=-1.0)
        layer(HIGH, HALF, S)
        layer(HIGH, 0, HALF)
        s_high = fresh("s_high", HALF)
        acc = next_bank()
        product(acc, GATE, HIGH, HALF, S, True)
        nc.scalar.activation(s_high, acc[:], ACT.Sigmoid, scale=-1.0)
        last_gate = next_bank()
        product(last_gate, GATE, HIGH, 0, HALF, True)

        d_low = fresh("d_low", ON_GPSIMD)
        for a in range(0, ON_GPSIMD, PIECE):
            cols = slice(a, a + PIECE)
            nc.vector.tensor_tensor(
                d_low[:, cols], res_rows[LOW][:].indirect(entries(a, a + PIECE)), neg_y[LOW][:, cols], ALU.add
            )
        for a, b in ((0, HALF), (HALF, ON_GPSIMD)):
            weighed = fresh("weighed_low%d" % a, b - a)
            nc.gpsimd.tensor_tensor(weighed, s_low[:, a:b], d_low[:, a:b], ALU.mult)
            result = fresh("result_low%d" % a, b - a)
            nc.gpsimd.tensor_tensor(result, weighed, neg_y[LOW][:, a:b], ALU.subtract)
            nc.sync.dma_start(out=out[0:P, a:b], in_=result)

        def turn(bank, src, first, last):
            blocks = PIECE // P
            for block in range(blocks):
                cols = slice(block * P, (block + 1) * P)
                nc.tensor.matmul(
                    bank[:, cols], src[:, cols], ident[:], is_transpose=True,
                    start=(first and block == 0), stop=(last and block == blocks - 1),
                )

        diff = {}
        back = {}

        def open_difference(rows, a, bank):
            diff[rows, a] = bank
            turn(bank, neg_y[rows][:, a : a + PIECE], True, False)

        def close_difference(rows, a, scalar_share):
            r = fresh("r%d_%d" % (rows, a), PIECE)
            if scalar_share < PIECE:
                window = res_rows[rows][:].indirect(entries(a + scalar_share, a + PIECE))
                nc.vector.tensor_copy(out=r[:, scalar_share:PIECE], in_=window)
            if scalar_share > 0:
                window = res_rows[rows][:].indirect(entries(a, a + scalar_share))
                nc.scalar.activation(r[:, 0:scalar_share], window, ACT.Copy)
            turn(diff[rows, a], r, False, True)

        def store(rows, a, result):
            nc.sync.dma_start(out=out[rows * P : (rows + 1) * P, a : a + PIECE], in_=result)

        def weigh_by_s(rows, a, s, weighed, bank):
            nc.vector.tensor_tensor(weighed, s, diff[rows, a][:, 0:PIECE], ALU.mult)
            back[rows, a] = bank
            turn(bank, weighed, True, True)

        def finish_by_s(rows, a):
            result = fresh("result%d_%d" % (rows, a), PIECE)
            nc.vector.scalar_tensor_tensor(
                out=result, in0=neg_y[rows][:, a : a + PIECE], scalar=-1.0, in1=back[rows, a][:, 0:PIECE],
                op0=ALU.mult, op1=ALU.add,
            )
            store(rows, a, result)

        def weigh_by_t(rows, a, t, weighed, bank):
            nc.vector.scalar_tensor_tensor(
                out=weighed, in0=t, scalar=-1.0, in1=diff[rows, a][:, 0:PIECE], op0=ALU.add, op1=ALU.mult
            )
            back[rows, a] = bank
            turn(bank, weighed, True, True)

        def finish_by_t(rows, a):
            result = fresh("result%d_%d" % (rows, a), PIECE)
            nc.vector.scalar_tensor_tensor(
                out=result, in0=back[rows, a][:, 0:PIECE], scalar=-0.5, in1=neg_y[rows][:, a : a + PIECE],
                op0=ALU.mult, op1=ALU.subtract,
            )
            store(rows, a, result)

        open_difference(LOW, ON_GPSIMD, own_bank("diff_low", "bank_a"))
        close_difference(LOW, ON_GPSIMD, 0)
        open_difference(HIGH, HALF, own_bank("diff_high2", "bank_c"))
        open_difference(HIGH, HALF + PIECE, own_bank("diff_high3", "bank_d"))
        open_difference(HIGH, 0, next_bank())
        open_difference(HIGH, PIECE, next_bank())
        close_difference(HIGH, HALF, 0)
        close_difference(HIGH, HALF + PIECE, 0)
        close_difference(HIGH, 0, PIECE)
        close_difference(HIGH, PIECE, P)

        late = fresh("late", HALF + PIECE, tag="r%d_%d" % (HIGH, HALF))
        t_high = late[:, 0:HALF]
        for a in range(0, HALF, PIECE):
            cols = slice(a, a + PIECE)
            nc.scalar.activation(t_high[:, cols], last_gate[:, cols], ACT.Tanh, scale=one_half[:])

        weigh_by_s(LOW, ON_GPSIMD, s_low[:, ON_GPSIMD:S], late[:, HALF:], own_bank("back_low", "bank_b"))
        weigh_by_s(HIGH, HALF, s_high[:, 0:PIECE], fresh("weighed2", PIECE), next_bank())
        weigh_by_s(HIGH, HALF + PIECE, s_high[:, PIECE:HALF], fresh("weighed3", PIECE), own_bank("back3", "bank_a"))
        finish_by_s(LOW, ON_GPSIMD)
        weigh_by_t(HIGH, 0, t_high[:, 0:PIECE], fresh("weighed0", PIECE), own_bank("back0", "bank_c"))
        weigh_by_t(HIGH, PIECE, t_high[:, PIECE:HALF], fresh("weighed1", PIECE), own_bank("back1", "bank_d"))
        finish_by_s(HIGH, HALF)
        finish_by_s(HIGH, HALF + PIECE)
        finish_by_t(HIGH, 0)
        finish_by_t(HIGH, PIECE)
